import numpy as np
import ml_dtypes


def mxq(x, axis, fmt="e4m3"):
    dtype, down = {"e4m3": (ml_dtypes.float8_e4m3fn, 7), "e5m2": (ml_dtypes.float8_e5m2, 14)}[fmt]
    v = np.moveaxis(np.asarray(x, np.float32).astype(ml_dtypes.bfloat16).astype(np.float64), axis, -1)
    blocks = v.reshape(v.shape[:-1] + (-1, 32))
    amax = np.abs(blocks).max(-1, keepdims=True)
    byte = np.maximum(np.where(amax > 0, np.frexp(amax)[1] - 1 + 127, 0) - down, 1)
    scale = np.exp2(byte - 127.0)
    codes = (blocks / scale).astype(np.float32).astype(dtype).astype(np.float64)
    return np.moveaxis((codes * scale).reshape(v.shape), -1, axis)


WIDE = False


def mx_kscale(k, group=512):
    if not WIDE:
        return np.ones(k)
    levels = np.array([18, -18])
    if group != 512:
        return np.exp2(np.random.permutation(np.resize(levels, k // group))).repeat(group)
    if k % 512:
        return np.exp2(np.random.permutation(np.resize(levels, k // 32))).repeat(32)
    a = np.empty((k // 512, 16))
    for p in range(k // 512):
        a[p, :8] = np.random.permutation(np.resize(levels, 8))
        for g in range(8):
            far = levels[np.abs(levels - a[p, g]) >= 10]
            a[p, g + 8] = far[np.random.randint(len(far))]
    return np.exp2(a.ravel()).repeat(32)


def f64(x):
    return np.asarray(x).astype(np.float64)


def bf(x):
    return np.asarray(x, np.float32).astype(ml_dtypes.bfloat16)


def planes(Y):
    r, m = Y.shape
    b = f64(bf(Y)).reshape(r // 32, 32, m)
    amax = np.abs(b).max(1)
    byte = np.clip(np.where(amax > 0, np.frexp(amax)[1] - 1 + 127 - 7, 1), 1, 254)
    codes = (b * np.exp2(127.0 - byte)[:, None, :]).reshape(r, m).astype(np.float32).astype(ml_dtypes.float8_e4m3fn).view(np.uint8)
    words = codes.reshape(r // 512, 128, 4, m).transpose(0, 1, 3, 2)
    return np.ascontiguousarray(words), np.ascontiguousarray(byte.astype(np.uint8).reshape(r // 512, 16, m))


G, D, M, N = 4, 128, 128, 512


def setup_inputs():
    n = np.random.standard_normal
    s_d = mx_kscale(D, 0)
    return {
        "x": (n((G, D, N)) * s_d[:, None]).astype(np.float32),
        "w": (np.where(np.arange(D)[:, None] <= np.arange(M)[None], 0.97 ** (np.arange(M)[None] - np.arange(D)[:, None]), 0.0) * 0.2 / s_d[:, None]).astype(np.float32),
        "dd": (np.random.uniform(0.5, 2.0, (1, N))).astype(np.float32),
        "xs": (n((G, M, N))).astype(np.float32),
        "x1": (n((G, M, N))).astype(np.float32),
    }


def reference(x, w, dd, xs, x1):
    wq = mxq(f64(w), 0, "e4m3")
    xq = mxq(f64(x), 1, "e4m3")
    z = wq.T @ xq
    y = (z + f64(dd) * f64(xs)) * f64(x1)
    Y = y.reshape(G * M, N)
    words, scales = planes(Y)
    return Y, words, scales

@@ -1,0 +1,199 @@
+from contextlib import ExitStack
+
+import concourse.mybir as mybir
+
+G, D, M, N = 4, 128, 128, 512
+FLOPS = 2 * G * D * M * N
+
+F32 = mybir.dt.float32
+BF16 = mybir.dt.bfloat16
+I32 = mybir.dt.int32
+U32 = mybir.dt.uint32
+U8 = mybir.dt.uint8
+FP8X4 = mybir.dt.float8_e4m3fn_x4
+ADD = mybir.AluOpType.add
+MULT = mybir.AluOpType.mult
+
+P = 128
+R = 32
+PACK = 4
+TILES = 4
+C = N // TILES
+
+
+def interleave(engine_copy, dst, src):
+    engine_copy(
+        out=dst[:].rearrange("p (c i) j -> p c j i", i=4),
+        in_=src[:].rearrange("p j (c i) -> p c j i", i=4),
+    )
+
+
+def tile_rows_pl_mix_hyena_kernel(tc, x, w, dd, xs, x1, out_0, out_1, out_2):
+    nc = tc.nc
+    xs_rows = xs.rearrange("g (i u) n -> (g i) u n", u=PACK)
+    x1_rows = x1.rearrange("g (i u) n -> (g i) u n", u=PACK)
+    y_rows = out_0.rearrange("(p u) n -> p u n", u=PACK)
+    words_out = out_1.rearrange("v p n u -> (v p) (n u)").bitcast(I32)
+    scales_out = out_2.rearrange("v f n -> (v f) n").bitcast(I32)
+
+    with ExitStack() as ctx:
+        sb = ctx.enter_context(tc.tile_pool(name="sb", bufs=1))
+        ps = ctx.enter_context(tc.psum_pool(name="ps", bufs=1))
+        ctx.enter_context(tc.manual_schedule())
+
+        w_raw = sb.tile([P, PACK, M], F32, name="w_raw")
+        w_bf = sb.tile([P, PACK, 4, R, PACK], BF16, name="w_bf", align_bytes=64)
+        w_codes = sb.tile([P, 20 * R], U32, name="w_codes", align_bytes=64)
+        w_scales = sb.tile([P, 20 * R], U8, name="w_scales", align_bytes=64)
+        w_scales_odd = sb.tile([P, 18 * R], U8, name="w_scales_odd", align_bytes=64)
+        dd_rows = sb.tile([P, R], F32, name="dd_rows", align_bytes=64)
+        dd_cols = sb.tile([P, R], F32, name="dd_cols", align_bytes=64)
+        dd_wide = sb.tile([P, N], F32, name="dd_wide", align_bytes=64)
+        dd_all = sb.tile([P, N], F32, name="dd_all", align_bytes=64)
+        x_raw = [sb.tile([P, PACK, C], F32, name="x_raw%d" % g) for g in range(G)]
+        x_bf = [sb.tile([P, C, PACK], BF16, name="x_bf%d" % g, align_bytes=64) for g in range(G)]
+        x_codes = [sb.tile([P, C], U32, name="x_codes%d" % g, align_bytes=64) for g in range(G)]
+        x_scales = [sb.tile([P, C], U8, name="x_scales%d" % g, align_bytes=64) for g in range(G)]
+        xs_sb = [sb.tile([P, 2, N], F32, name="xs%d" % h) for h in range(2)]
+        direct = [sb.tile([P, 2, N], F32, name="direct%d" % h) for h in range(2)]
+        x1_sb = [sb.tile([P, PACK, 2 * C], F32, name="x1_%d" % h) for h in range(2)]
+        summed = [sb.tile([P, PACK, C], F32, name="summed%d" % r) for r in range(TILES)]
+        y = [sb.tile([P, PACK, C], F32, name="y%d" % r) for r in range(TILES)]
+        y_bf = [sb.tile([P, C, PACK], BF16, name="y_bf%d" % r, align_bytes=64) for r in range(TILES)]
+        y_codes = sb.tile([P, N], U32, name="y_codes", align_bytes=64)
+        y_scales = sb.tile([P, N], U8, name="y_scales", align_bytes=64)
+        bank = [[ps.tile([P, PACK, C], F32, name="z%d_%d" % (r, h)) for h in range(2)] for r in range(TILES)]
+
+        nc.scalar.dma_start(
+            out=dd_rows[:],
+            in_=dd.rearrange("o (b i) -> o b i", i=R).broadcast_to([P // 16, 16, R]),
+        )
+        nc.scalar.dma_start(out=xs_sb[0][:], in_=xs_rows[:, 0:2, :])
+        w_rows = w.rearrange("(p j) m -> p j m", j=PACK)
+        for r in range(TILES):
+            nc.sync.dma_start(out=w_raw[R * r : R * (r + 1)], in_=w_rows)
+        for g in range(G):
+            for r in range(TILES):
+                x_rows = x[(r + g) % G].rearrange("(p j) n -> p j n", j=PACK)
+                nc.sync.dma_start(out=x_raw[g][R * r : R * (r + 1)], in_=x_rows[:, :, C * r : C * (r + 1)])
+        nc.sync.dma_start(out=xs_sb[1][:], in_=xs_rows[:, 2:4, :])
+        for h in range(2):
+            nc.sync.dma_start(out=x1_sb[h][:], in_=x1_rows[:, :, 2 * C * h : 2 * C * (h + 1)])
+
+        nc.vector.memset(w_bf[:], 0.0)
+        nc.vector.memset(w_codes[:, 16 * R :], 0)
+        nc.vector.memset(w_scales[:].bitcast(I32), 0)
+
+        for g in range(G):
+            interleave(nc.scalar.copy, x_bf[g], x_raw[g])
+
+        def quantize_x(g):
+            nc.vector.quantize_mx(
+                out=x_codes[g][:].bitcast(FP8X4),
+                scales=x_scales[g][:],
+                in_=x_bf[g][:].rearrange("p c j -> p (c j)"),
+            )
+
+        def direct_term(h):
+            nc.vector.tensor_tensor(
+                out=direct[h][:],
+                in0=xs_sb[h][:],
+                in1=dd_all[:].unsqueeze(1).to_broadcast([P, 2, N]),
+                op=MULT,
+            )
+
+        nc.vector.tensor_copy(out=w_bf[:, :, 3], in_=w_raw[:].rearrange("p j (i u) -> p u i j", u=PACK))
+        nc.vector.transpose(out=dd_cols[:], in_=dd_rows[:])
+        nc.vector.quantize_mx(
+            out=w_codes[:, : 16 * R].bitcast(FP8X4),
+            scales=w_scales[:, : 16 * R],
+            in_=w_bf[:].rearrange("p u b i j -> p (u b i j)"),
+        )
+        nc.vector.tensor_copy(
+            out=dd_wide[:].rearrange("p (b i) -> p b i", i=R),
+            in_=dd_cols[:, 0:16].unsqueeze(2).to_broadcast([P, 16, R]),
+        )
+        nc.vector.tensor_copy(out=w_scales_odd[:].bitcast(I32), in_=w_scales[:, R : 19 * R].bitcast(I32))
+        quantize_x(0)
+        nc.vector.transpose(out=dd_all[:], in_=dd_wide[:])
+        quantize_x(1)
+        direct_term(0)
+        quantize_x(2)
+        quantize_x(3)
+        direct_term(1)
+
+        def product(r, u, g):
+            rows = slice(R * r, R * (r + 1))
+            block = 4 * u + 3 - (r + g) % G
+            cols = slice(R * block, R * block + M)
+            if block % 2 == 0:
+                scale = w_scales[rows, cols]
+            else:
+                scale = w_scales_odd[rows, R * (block - 1) : R * (block - 1) + M]
+            nc.tensor.matmul_mx(
+                out=bank[r][u // 2][:, u % 2, :],
+                lhsT=w_codes[rows, cols].bitcast(FP8X4),
+                lhsT_scale=scale,
+                rhs=x_codes[g][rows, :].bitcast(FP8X4),
+                rhs_scale=x_scales[g][rows, :],
+                start=(g == 0),
+                stop=(g == G - 1),
+            )
+
+        for g in range(G):
+            for u in (0, 2):
+                for r in range(TILES):
+                    product(r, u, g)
+        for u in (1, 3):
+            for g in range(G):
+                for r in range(TILES):
+                    product(r, u, g)
+
+        def add_direct(r, h):
+            nc.vector.tensor_tensor(
+                out=summed[r][:, 2 * h : 2 * h + 2, :],
+                in0=bank[r][h][:, 0:2, :],
+                in1=direct[h][:, :, C * r : C * (r + 1)],
+                op=ADD,
+            )
+
+        def gate(r):
+            nc.vector.tensor_tensor(
+                out=y[r][:],
+                in0=summed[r][:],
+                in1=x1_sb[r // 2][:, :, C * (r % 2) : C * (r % 2 + 1)],
+                op=MULT,
+            )
+            nc.sync.dma_start(out=y_rows[:, :, C * r : C * (r + 1)], in_=y[r][:])
+            interleave(nc.scalar.copy, y_bf[r], y[r])
+
+        def quantize_y(r):
+            nc.vector.quantize_mx(
+                out=y_codes[:, C * r : C * (r + 1)].bitcast(FP8X4),
+                scales=y_scales[:, C * r : C * (r + 1)],
+                in_=y_bf[r][:].rearrange("p c u -> p (c u)"),
+            )
+
+        def store_words(h):
+            cols = slice(2 * C * h, 2 * C * (h + 1))
+            nc.sync.dma_start(out=words_out[:, cols], in_=y_codes[:, cols].bitcast(I32))
+
+        for r in range(TILES):
+            add_direct(r, 0)
+        add_direct(0, 1)
+        add_direct(1, 1)
+        gate(0)
+        add_direct(2, 1)
+        gate(1)
+        add_direct(3, 1)
+        gate(2)
+        quantize_y(0)
+        gate(3)
+        quantize_y(1)
+        store_words(0)
+        quantize_y(2)
+        quantize_y(3)
+        store_words(1)
+        for q in range(4):
+            queue = nc.sync if q % 2 == 0 else nc.scalar
+            queue.dma_start(out=scales_out[4 * q : 4 * q + 4, :], in_=y_scales[R * q : R * q + 4, :].bitcast(I32))

@@ -17,22 +17,21 @@ MULT = mybir.AluOpType.mult
 P = 128
 R = 32
 PACK = 4
-TILES = 4
-C = N // TILES
+H = N // 2
 
 
 def interleave(engine_copy, dst, src):
     engine_copy(
-        out=dst[:].rearrange("p (c i) j -> p c j i", i=4),
-        in_=src[:].rearrange("p j (c i) -> p c j i", i=4),
+        out=dst.rearrange("p (c i) j -> p c j i", i=4),
+        in_=src.rearrange("p j (c i) -> p c j i", i=4),
     )
 
 
 def tile_rows_pl_mix_hyena_kernel(tc, x, w, dd, xs, x1, out_0, out_1, out_2):
     nc = tc.nc
-    xs_rows = xs.rearrange("g (i u) n -> (g i) u n", u=PACK)
-    x1_rows = x1.rearrange("g (i u) n -> (g i) u n", u=PACK)
-    y_rows = out_0.rearrange("(p u) n -> p u n", u=PACK)
+    x_rows = x.rearrange("g (p j) n -> (g p) j n", j=PACK)
+    w_rows = w.rearrange("(p j) m -> p j m", j=PACK)
+    y_rows = out_0.rearrange("(g m) n -> g m n", g=G)
     words_out = out_1.rearrange("v p n u -> (v p) (n u)").bitcast(I32)
     scales_out = out_2.rearrange("v f n -> (v f) n").bitcast(I32)
 
@@ -42,158 +41,114 @@ def tile_rows_pl_mix_hyena_kernel(tc, x, w, dd, xs, x1, out_0, out_1, out_2):
         ctx.enter_context(tc.manual_schedule())
 
         w_raw = sb.tile([P, PACK, M], F32, name="w_raw")
-        w_bf = sb.tile([P, PACK, 4, R, PACK], BF16, name="w_bf", align_bytes=64)
-        w_codes = sb.tile([P, 20 * R], U32, name="w_codes", align_bytes=64)
-        w_scales = sb.tile([P, 20 * R], U8, name="w_scales", align_bytes=64)
-        w_scales_odd = sb.tile([P, 18 * R], U8, name="w_scales_odd", align_bytes=64)
+        w_bf = sb.tile([P, M, PACK], BF16, name="w_bf", align_bytes=64)
+        w_codes = sb.tile([P, M], U32, name="w_codes", align_bytes=64)
+        w_scales = sb.tile([P, M], U8, name="w_scales", align_bytes=64)
         dd_rows = sb.tile([P, R], F32, name="dd_rows", align_bytes=64)
         dd_cols = sb.tile([P, R], F32, name="dd_cols", align_bytes=64)
         dd_wide = sb.tile([P, N], F32, name="dd_wide", align_bytes=64)
         dd_all = sb.tile([P, N], F32, name="dd_all", align_bytes=64)
-        x_raw = [sb.tile([P, PACK, C], F32, name="x_raw%d" % g) for g in range(G)]
-        x_bf = [sb.tile([P, C, PACK], BF16, name="x_bf%d" % g, align_bytes=64) for g in range(G)]
-        x_codes = [sb.tile([P, C], U32, name="x_codes%d" % g, align_bytes=64) for g in range(G)]
-        x_scales = [sb.tile([P, C], U8, name="x_scales%d" % g, align_bytes=64) for g in range(G)]
-        xs_sb = [sb.tile([P, 2, N], F32, name="xs%d" % h) for h in range(2)]
-        direct = [sb.tile([P, 2, N], F32, name="direct%d" % h) for h in range(2)]
-        x1_sb = [sb.tile([P, PACK, 2 * C], F32, name="x1_%d" % h) for h in range(2)]
-        summed = [sb.tile([P, PACK, C], F32, name="summed%d" % r) for r in range(TILES)]
-        y = [sb.tile([P, PACK, C], F32, name="y%d" % r) for r in range(TILES)]
-        y_bf = [sb.tile([P, C, PACK], BF16, name="y_bf%d" % r, align_bytes=64) for r in range(TILES)]
+        x_raw = [sb.tile([P, PACK, H], F32, name="x_raw%d" % h) for h in range(2)]
+        x_bf = [sb.tile([P, H, PACK], BF16, name="x_bf%d" % h, align_bytes=64) for h in range(2)]
+        x_codes = sb.tile([P, N], U32, name="x_codes", align_bytes=64)
+        x_scales = sb.tile([P, N], U8, name="x_scales", align_bytes=64)
+        xs_sb = [sb.tile([P, N], F32, name="xs%d" % g) for g in range(G)]
+        x1_sb = [sb.tile([P, N], F32, name="x1_%d" % g) for g in range(G)]
+        direct = [sb.tile([P, N], F32, name="direct%d" % g) for g in range(G)]
+        summed = [sb.tile([P, N], F32, name="summed%d" % g) for g in range(G)]
+        y = [sb.tile([P, N], F32, name="y%d" % g) for g in range(G)]
+        y_bf = [sb.tile([P, N], BF16, name="y_bf%d" % g) for g in range(G)]
+        y_moved = sb.tile([P, PACK, N], BF16, name="y_moved")
+        y_words = [sb.tile([P, H, PACK], BF16, name="y_words%d" % h, align_bytes=64) for h in range(2)]
         y_codes = sb.tile([P, N], U32, name="y_codes", align_bytes=64)
         y_scales = sb.tile([P, N], U8, name="y_scales", align_bytes=64)
-        bank = [[ps.tile([P, PACK, C], F32, name="z%d_%d" % (r, h)) for h in range(2)] for r in range(TILES)]
+        z = [ps.tile([P, N], F32, name="z%d" % g) for g in range(G)]
 
         nc.scalar.dma_start(
             out=dd_rows[:],
             in_=dd.rearrange("o (b i) -> o b i", i=R).broadcast_to([P // 16, 16, R]),
         )
-        nc.scalar.dma_start(out=xs_sb[0][:], in_=xs_rows[:, 0:2, :])
-        w_rows = w.rearrange("(p j) m -> p j m", j=PACK)
-        for r in range(TILES):
-            nc.sync.dma_start(out=w_raw[R * r : R * (r + 1)], in_=w_rows)
         for g in range(G):
-            for r in range(TILES):
-                x_rows = x[(r + g) % G].rearrange("(p j) n -> p j n", j=PACK)
-                nc.sync.dma_start(out=x_raw[g][R * r : R * (r + 1)], in_=x_rows[:, :, C * r : C * (r + 1)])
-        nc.sync.dma_start(out=xs_sb[1][:], in_=xs_rows[:, 2:4, :])
+            queue = nc.sync if g < 2 else nc.scalar
+            queue.dma_start(out=w_raw[R * g : R * (g + 1)], in_=w_rows)
         for h in range(2):
-            nc.sync.dma_start(out=x1_sb[h][:], in_=x1_rows[:, :, 2 * C * h : 2 * C * (h + 1)])
-
-        nc.vector.memset(w_bf[:], 0.0)
-        nc.vector.memset(w_codes[:, 16 * R :], 0)
-        nc.vector.memset(w_scales[:].bitcast(I32), 0)
-
+            nc.sync.dma_start(out=x_raw[h][:], in_=x_rows[:, :, H * h : H * (h + 1)])
         for g in range(G):
-            interleave(nc.scalar.copy, x_bf[g], x_raw[g])
+            nc.sync.dma_start(out=xs_sb[g][:], in_=xs[g])
+            nc.sync.dma_start(out=x1_sb[g][:], in_=x1[g])
 
-        def quantize_x(g):
+        def quantize(codes, scales, src, cols):
             nc.vector.quantize_mx(
-                out=x_codes[g][:].bitcast(FP8X4),
-                scales=x_scales[g][:],
-                in_=x_bf[g][:].rearrange("p c j -> p (c j)"),
+                out=codes[:, cols].bitcast(FP8X4),
+                scales=scales[:, cols],
+                in_=src.rearrange("p c j -> p (c j)"),
             )
 
-        def direct_term(h):
-            nc.vector.tensor_tensor(
-                out=direct[h][:],
-                in0=xs_sb[h][:],
-                in1=dd_all[:].unsqueeze(1).to_broadcast([P, 2, N]),
-                op=MULT,
-            )
-
-        nc.vector.tensor_copy(out=w_bf[:, :, 3], in_=w_raw[:].rearrange("p j (i u) -> p u i j", u=PACK))
+        interleave(nc.scalar.copy, x_bf[0][:], x_raw[0][:])
         nc.vector.transpose(out=dd_cols[:], in_=dd_rows[:])
-        nc.vector.quantize_mx(
-            out=w_codes[:, : 16 * R].bitcast(FP8X4),
-            scales=w_scales[:, : 16 * R],
-            in_=w_bf[:].rearrange("p u b i j -> p (u b i j)"),
-        )
+        interleave(nc.vector.tensor_copy, w_bf[:], w_raw[:])
         nc.vector.tensor_copy(
             out=dd_wide[:].rearrange("p (b i) -> p b i", i=R),
             in_=dd_cols[:, 0:16].unsqueeze(2).to_broadcast([P, 16, R]),
         )
-        nc.vector.tensor_copy(out=w_scales_odd[:].bitcast(I32), in_=w_scales[:, R : 19 * R].bitcast(I32))
-        quantize_x(0)
+        quantize(w_codes, w_scales, w_bf[:], slice(0, M))
+        split = 160
+        interleave(nc.vector.tensor_copy, x_bf[1][:, :split, :], x_raw[1][:, :, :split])
+        interleave(nc.scalar.copy, x_bf[1][:, split:, :], x_raw[1][:, :, split:])
+        quantize(x_codes, x_scales, x_bf[0][:], slice(0, H))
+        quantize(x_codes, x_scales, x_bf[1][:], slice(H, N))
         nc.vector.transpose(out=dd_all[:], in_=dd_wide[:])
-        quantize_x(1)
-        direct_term(0)
-        quantize_x(2)
-        quantize_x(3)
-        direct_term(1)
-
-        def product(r, u, g):
-            rows = slice(R * r, R * (r + 1))
-            block = 4 * u + 3 - (r + g) % G
-            cols = slice(R * block, R * block + M)
-            if block % 2 == 0:
-                scale = w_scales[rows, cols]
-            else:
-                scale = w_scales_odd[rows, R * (block - 1) : R * (block - 1) + M]
-            nc.tensor.matmul_mx(
-                out=bank[r][u // 2][:, u % 2, :],
-                lhsT=w_codes[rows, cols].bitcast(FP8X4),
-                lhsT_scale=scale,
-                rhs=x_codes[g][rows, :].bitcast(FP8X4),
-                rhs_scale=x_scales[g][rows, :],
-                start=(g == 0),
-                stop=(g == G - 1),
-            )
 
         for g in range(G):
-            for u in (0, 2):
-                for r in range(TILES):
-                    product(r, u, g)
-        for u in (1, 3):
-            for g in range(G):
-                for r in range(TILES):
-                    product(r, u, g)
-
-        def add_direct(r, h):
-            nc.vector.tensor_tensor(
-                out=summed[r][:, 2 * h : 2 * h + 2, :],
-                in0=bank[r][h][:, 0:2, :],
-                in1=direct[h][:, :, C * r : C * (r + 1)],
-                op=ADD,
+            rows = slice(R * g, R * (g + 1))
+            nc.tensor.matmul_mx(
+                out=z[g][:],
+                lhsT=w_codes[rows, :].bitcast(FP8X4),
+                lhsT_scale=w_scales[rows, :],
+                rhs=x_codes[rows, :].bitcast(FP8X4),
+                rhs_scale=x_scales[rows, :],
+                start=True,
+                stop=True,
             )
 
-        def gate(r):
-            nc.vector.tensor_tensor(
-                out=y[r][:],
-                in0=summed[r][:],
-                in1=x1_sb[r // 2][:, :, C * (r % 2) : C * (r % 2 + 1)],
-                op=MULT,
-            )
-            nc.sync.dma_start(out=y_rows[:, :, C * r : C * (r + 1)], in_=y[r][:])
-            interleave(nc.scalar.copy, y_bf[r], y[r])
+        def direct_term(g):
+            nc.vector.tensor_tensor(out=direct[g][:], in0=xs_sb[g][:], in1=dd_all[:], op=MULT)
 
-        def quantize_y(r):
-            nc.vector.quantize_mx(
-                out=y_codes[:, C * r : C * (r + 1)].bitcast(FP8X4),
-                scales=y_scales[:, C * r : C * (r + 1)],
-                in_=y_bf[r][:].rearrange("p c u -> p (c u)"),
-            )
+        def add_direct(g):
+            nc.vector.tensor_tensor(out=summed[g][:], in0=z[g][:], in1=direct[g][:], op=ADD)
 
-        def store_words(h):
-            cols = slice(2 * C * h, 2 * C * (h + 1))
-            nc.sync.dma_start(out=words_out[:, cols], in_=y_codes[:, cols].bitcast(I32))
+        def gate(g):
+            nc.vector.tensor_tensor(out=y[g][:], in0=summed[g][:], in1=x1_sb[g][:], op=MULT)
+            nc.scalar.copy(out=y_bf[g][:], in_=y[g][:])
+            nc.scalar.dma_start(out=y_moved[R * g : R * (g + 1)], in_=y_bf[g][:])
+            nc.sync.dma_start(out=y_rows[g], in_=y[g][:])
 
-        for r in range(TILES):
-            add_direct(r, 0)
-        add_direct(0, 1)
-        add_direct(1, 1)
+        direct_term(0)
+        direct_term(1)
+        add_direct(0)
+        add_direct(1)
         gate(0)
-        add_direct(2, 1)
+        direct_term(2)
         gate(1)
-        add_direct(3, 1)
+        add_direct(2)
+        direct_term(3)
         gate(2)
-        quantize_y(0)
-        gate(3)
-        quantize_y(1)
-        store_words(0)
-        quantize_y(2)
-        quantize_y(3)
-        store_words(1)
+        add_direct(3)
+        last = G - 1
+        for h in range(2):
+            cols = slice(H * h, H * (h + 1))
+            nc.vector.tensor_tensor(out=y_bf[last][:, cols], in0=summed[last][:, cols], in1=x1_sb[last][:, cols], op=MULT)
+            nc.scalar.dma_start(out=y_moved[R * last :, :, cols], in_=y_bf[last][:, cols])
+        nc.vector.tensor_tensor(out=y[last][:], in0=summed[last][:], in1=x1_sb[last][:], op=MULT)
+        nc.sync.dma_start(out=y_rows[last], in_=y[last][:])
+
+        interleave(nc.vector.tensor_copy, y_words[0][:], y_moved[:, :, 0:H])
+        interleave(nc.scalar.copy, y_words[1][:, split:, :], y_moved[:, :, H + split :])
+        interleave(nc.vector.tensor_copy, y_words[1][:, :split, :], y_moved[:, :, H : H + split])
+        for h in range(2):
+            cols = slice(H * h, H * (h + 1))
+            quantize(y_codes, y_scales, y_words[h][:], cols)
+            nc.sync.dma_start(out=words_out[:, cols], in_=y_codes[:, cols].bitcast(I32))
         for q in range(4):
             queue = nc.sync if q % 2 == 0 else nc.scalar
             queue.dma_start(out=scales_out[4 * q : 4 * q + 4, :], in_=y_scales[R * q : R * q + 4, :].bitcast(I32))

@@ -31,7 +31,8 @@ def tile_rows_pl_mix_hyena_kernel(tc, x, w, dd, xs, x1, out_0, out_1, out_2):
     nc = tc.nc
     x_rows = x.rearrange("g (p j) n -> (g p) j n", j=PACK)
     w_rows = w.rearrange("(p j) m -> p j m", j=PACK)
-    y_rows = out_0.rearrange("(g m) n -> g m n", g=G)
+    y_rows = out_0.rearrange("(g m) n -> m g n", g=G)
+    x1_rows = x1.rearrange("g m n -> m g n")
     words_out = out_1.rearrange("v p n u -> (v p) (n u)").bitcast(I32)
     scales_out = out_2.rearrange("v f n -> (v f) n").bitcast(I32)
 
@@ -40,10 +41,11 @@ def tile_rows_pl_mix_hyena_kernel(tc, x, w, dd, xs, x1, out_0, out_1, out_2):
         ps = ctx.enter_context(tc.psum_pool(name="ps", bufs=1))
         ctx.enter_context(tc.manual_schedule())
 
-        w_raw = sb.tile([P, PACK, M], F32, name="w_raw")
-        w_bf = sb.tile([P, M, PACK], BF16, name="w_bf", align_bytes=64)
-        w_codes = sb.tile([P, M], U32, name="w_codes", align_bytes=64)
-        w_scales = sb.tile([P, M], U8, name="w_scales", align_bytes=64)
+        w_raw = sb.tile([R, PACK, M], F32, name="w_raw")
+        w_bf = sb.tile([R, M, PACK], BF16, name="w_bf", align_bytes=64)
+        w_mx = sb.tile([P, M + M // 4], I32, name="w_mx", align_bytes=64)
+        w_codes = w_mx[:, :M]
+        w_scales = w_mx[:, M:].bitcast(U8)
         dd_rows = sb.tile([P, R], F32, name="dd_rows", align_bytes=64)
         dd_cols = sb.tile([P, R], F32, name="dd_cols", align_bytes=64)
         dd_wide = sb.tile([P, N], F32, name="dd_wide", align_bytes=64)
@@ -53,29 +55,22 @@ def tile_rows_pl_mix_hyena_kernel(tc, x, w, dd, xs, x1, out_0, out_1, out_2):
         x_codes = sb.tile([P, N], U32, name="x_codes", align_bytes=64)
         x_scales = sb.tile([P, N], U8, name="x_scales", align_bytes=64)
         xs_sb = [sb.tile([P, N], F32, name="xs%d" % g) for g in range(G)]
-        x1_sb = [sb.tile([P, N], F32, name="x1_%d" % g) for g in range(G)]
+        x1_sb = [sb.tile([P, G, H], F32, name="x1_%d" % h) for h in range(2)]
         direct = [sb.tile([P, N], F32, name="direct%d" % g) for g in range(G)]
-        summed = [sb.tile([P, N], F32, name="summed%d" % g) for g in range(G)]
-        y = [sb.tile([P, N], F32, name="y%d" % g) for g in range(G)]
-        y_bf = [sb.tile([P, N], BF16, name="y_bf%d" % g) for g in range(G)]
-        y_moved = sb.tile([P, PACK, N], BF16, name="y_moved")
+        summed = sb.tile([P, G, N], F32, name="summed")
+        y = [sb.tile([P, G, H], F32, name="y%d" % h) for h in range(2)]
+        y_bf = [sb.tile([P, G, H], BF16, name="y_bf%d" % h) for h in range(2)]
+        y_moved = [sb.tile([P, PACK, H], BF16, name="y_moved%d" % h) for h in range(2)]
         y_words = [sb.tile([P, H, PACK], BF16, name="y_words%d" % h, align_bytes=64) for h in range(2)]
         y_codes = sb.tile([P, N], U32, name="y_codes", align_bytes=64)
         y_scales = sb.tile([P, N], U8, name="y_scales", align_bytes=64)
         z = [ps.tile([P, N], F32, name="z%d" % g) for g in range(G)]
 
+        nc.sync.dma_start(out=w_raw[:], in_=w_rows)
         nc.scalar.dma_start(
             out=dd_rows[:],
             in_=dd.rearrange("o (b i) -> o b i", i=R).broadcast_to([P // 16, 16, R]),
         )
-        for g in range(G):
-            queue = nc.sync if g < 2 else nc.scalar
-            queue.dma_start(out=w_raw[R * g : R * (g + 1)], in_=w_rows)
-        for h in range(2):
-            nc.sync.dma_start(out=x_raw[h][:], in_=x_rows[:, :, H * h : H * (h + 1)])
-        for g in range(G):
-            nc.sync.dma_start(out=xs_sb[g][:], in_=xs[g])
-            nc.sync.dma_start(out=x1_sb[g][:], in_=x1[g])
 
         def quantize(codes, scales, src, cols):
             nc.vector.quantize_mx(
@@ -84,20 +79,30 @@ def tile_rows_pl_mix_hyena_kernel(tc, x, w, dd, xs, x1, out_0, out_1, out_2):
                 in_=src.rearrange("p c j -> p (c j)"),
             )
 
-        interleave(nc.scalar.copy, x_bf[0][:], x_raw[0][:])
+        nc.vector.memset(w_mx[:R, M:], 0)
+        interleave(nc.scalar.copy, w_bf[:], w_raw[:])
         nc.vector.transpose(out=dd_cols[:], in_=dd_rows[:])
-        interleave(nc.vector.tensor_copy, w_bf[:], w_raw[:])
+        quantize(w_codes[:R], w_scales[:R], w_bf[:], slice(0, M))
+        for g in range(1, G):
+            nc.scalar.dma_start(out=w_mx[R * g : R * (g + 1)], in_=w_mx[:R])
+        for h in range(2):
+            nc.sync.dma_start(out=x_raw[h][:], in_=x_rows[:, :, H * h : H * (h + 1)])
+        for g in range(G):
+            nc.sync.dma_start(out=xs_sb[g][:], in_=xs[g])
+        for h in range(2):
+            nc.sync.dma_start(out=x1_sb[h][:], in_=x1_rows[:, :, H * h : H * (h + 1)])
+
+        interleave(nc.scalar.copy, x_bf[0][:], x_raw[0][:])
         nc.vector.tensor_copy(
             out=dd_wide[:].rearrange("p (b i) -> p b i", i=R),
             in_=dd_cols[:, 0:16].unsqueeze(2).to_broadcast([P, 16, R]),
         )
-        quantize(w_codes, w_scales, w_bf[:], slice(0, M))
+        nc.vector.transpose(out=dd_all[:], in_=dd_wide[:])
         split = 160
+        quantize(x_codes, x_scales, x_bf[0][:], slice(0, H))
         interleave(nc.vector.tensor_copy, x_bf[1][:, :split, :], x_raw[1][:, :, :split])
         interleave(nc.scalar.copy, x_bf[1][:, split:, :], x_raw[1][:, :, split:])
-        quantize(x_codes, x_scales, x_bf[0][:], slice(0, H))
         quantize(x_codes, x_scales, x_bf[1][:], slice(H, N))
-        nc.vector.transpose(out=dd_all[:], in_=dd_wide[:])
 
         for g in range(G):
             rows = slice(R * g, R * (g + 1))
@@ -115,40 +120,43 @@ def tile_rows_pl_mix_hyena_kernel(tc, x, w, dd, xs, x1, out_0, out_1, out_2):
             nc.vector.tensor_tensor(out=direct[g][:], in0=xs_sb[g][:], in1=dd_all[:], op=MULT)
 
         def add_direct(g):
-            nc.vector.tensor_tensor(out=summed[g][:], in0=z[g][:], in1=direct[g][:], op=ADD)
+            nc.vector.tensor_tensor(out=summed[:, g, :], in0=z[g][:], in1=direct[g][:], op=ADD)
 
-        def gate(g):
-            nc.vector.tensor_tensor(out=y[g][:], in0=summed[g][:], in1=x1_sb[g][:], op=MULT)
-            nc.scalar.copy(out=y_bf[g][:], in_=y[g][:])
-            nc.scalar.dma_start(out=y_moved[R * g : R * (g + 1)], in_=y_bf[g][:])
-            nc.sync.dma_start(out=y_rows[g], in_=y[g][:])
+        def gate(out, h, groups):
+            nc.vector.tensor_tensor(
+                out=out[:, groups, :], in0=summed[:, groups, H * h : H * (h + 1)], in1=x1_sb[h][:, groups, :], op=MULT
+            )
+
+        def move(h, g):
+            queue = nc.sync if g < 2 else nc.scalar
+            queue.dma_start(out=y_moved[h][R * g : R * (g + 1)], in_=y_bf[h][:, g, :])
+
+        def planes(h):
+            cols = slice(H * h, H * (h + 1))
+            quantize(y_codes, y_scales, y_words[h][:], cols)
+            nc.sync.dma_start(out=words_out[:, cols], in_=y_codes[:, cols].bitcast(I32))
 
         direct_term(0)
         direct_term(1)
         add_direct(0)
-        add_direct(1)
-        gate(0)
         direct_term(2)
-        gate(1)
-        add_direct(2)
+        add_direct(1)
         direct_term(3)
-        gate(2)
+        add_direct(2)
         add_direct(3)
-        last = G - 1
         for h in range(2):
-            cols = slice(H * h, H * (h + 1))
-            nc.vector.tensor_tensor(out=y_bf[last][:, cols], in0=summed[last][:, cols], in1=x1_sb[last][:, cols], op=MULT)
-            nc.scalar.dma_start(out=y_moved[R * last :, :, cols], in_=y_bf[last][:, cols])
-        nc.vector.tensor_tensor(out=y[last][:], in0=summed[last][:], in1=x1_sb[last][:], op=MULT)
-        nc.sync.dma_start(out=y_rows[last], in_=y[last][:])
-
-        interleave(nc.vector.tensor_copy, y_words[0][:], y_moved[:, :, 0:H])
-        interleave(nc.scalar.copy, y_words[1][:, split:, :], y_moved[:, :, H + split :])
-        interleave(nc.vector.tensor_copy, y_words[1][:, :split, :], y_moved[:, :, H : H + split])
+            for g in (0, 2):
+                gate(y_bf[h], h, slice(g, g + 2))
+                move(h, g)
+                move(h, g + 1)
         for h in range(2):
-            cols = slice(H * h, H * (h + 1))
-            quantize(y_codes, y_scales, y_words[h][:], cols)
-            nc.sync.dma_start(out=words_out[:, cols], in_=y_codes[:, cols].bitcast(I32))
+            gate(y[h], h, slice(0, G))
+            nc.sync.dma_start(out=y_rows[:, :, H * h : H * (h + 1)], in_=y[h][:])
+        interleave(nc.scalar.copy, y_words[0][:], y_moved[0][:])
+        planes(0)
+        interleave(nc.vector.tensor_copy, y_words[1][:, :split, :], y_moved[1][:, :, :split])
+        interleave(nc.scalar.copy, y_words[1][:, split:, :], y_moved[1][:, :, split:])
+        planes(1)
         for q in range(4):
             queue = nc.sync if q % 2 == 0 else nc.scalar
             queue.dma_start(out=scales_out[4 * q : 4 * q + 4, :], in_=y_scales[R * q : R * q + 4, :].bitcast(I32))

@@ -83,10 +83,10 @@ def tile_rows_pl_mix_hyena_kernel(tc, x, w, dd, xs, x1, out_0, out_1, out_2):
         interleave(nc.scalar.copy, w_bf[:], w_raw[:])
         nc.vector.transpose(out=dd_cols[:], in_=dd_rows[:])
         quantize(w_codes[:R], w_scales[:R], w_bf[:], slice(0, M))
-        for g in range(1, G):
-            nc.scalar.dma_start(out=w_mx[R * g : R * (g + 1)], in_=w_mx[:R])
         for h in range(2):
             nc.sync.dma_start(out=x_raw[h][:], in_=x_rows[:, :, H * h : H * (h + 1)])
+        for g in range(1, G):
+            nc.sync.dma_start(out=w_mx[R * g : R * (g + 1)], in_=w_mx[:R])
         for g in range(G):
             nc.sync.dma_start(out=xs_sb[g][:], in_=xs[g])
         for h in range(2):
@@ -127,9 +127,11 @@ def tile_rows_pl_mix_hyena_kernel(tc, x, w, dd, xs, x1, out_0, out_1, out_2):
                 out=out[:, groups, :], in0=summed[:, groups, H * h : H * (h + 1)], in1=x1_sb[h][:, groups, :], op=MULT
             )
 
-        def move(h, g):
-            queue = nc.sync if g < 2 else nc.scalar
+        def move(queue, h, g):
             queue.dma_start(out=y_moved[h][R * g : R * (g + 1)], in_=y_bf[h][:, g, :])
+
+        def store_y(h):
+            nc.sync.dma_start(out=y_rows[:, :, H * h : H * (h + 1)], in_=y[h][:])
 
         def planes(h):
             cols = slice(H * h, H * (h + 1))
@@ -144,18 +146,22 @@ def tile_rows_pl_mix_hyena_kernel(tc, x, w, dd, xs, x1, out_0, out_1, out_2):
         direct_term(3)
         add_direct(2)
         add_direct(3)
+        for g in (0, 2):
+            gate(y[0], 0, slice(g, g + 2))
+            nc.scalar.copy(out=y_bf[0][:, g : g + 2, :], in_=y[0][:, g : g + 2, :])
+            move(nc.sync, 0, g)
+            move(nc.sync, 0, g + 1)
+        for g, queue in ((0, nc.scalar), (2, nc.sync)):
+            gate(y_bf[1], 1, slice(g, g + 2))
+            move(queue, 1, g)
+            move(queue, 1, g + 1)
+        store_y(0)
+        gate(y[1], 1, slice(0, G))
+        store_y(1)
         for h in range(2):
-            for g in (0, 2):
-                gate(y_bf[h], h, slice(g, g + 2))
-                move(h, g)
-                move(h, g + 1)
-        for h in range(2):
-            gate(y[h], h, slice(0, G))
-            nc.sync.dma_start(out=y_rows[:, :, H * h : H * (h + 1)], in_=y[h][:])
-        interleave(nc.scalar.copy, y_words[0][:], y_moved[0][:])
+            interleave(nc.vector.tensor_copy, y_words[h][:, :split, :], y_moved[h][:, :, :split])
+            interleave(nc.scalar.copy, y_words[h][:, split:, :], y_moved[h][:, :, split:])
         planes(0)
-        interleave(nc.vector.tensor_copy, y_words[1][:, :split, :], y_moved[1][:, :, :split])
-        interleave(nc.scalar.copy, y_words[1][:, split:, :], y_moved[1][:, :, split:])
         planes(1)
         for q in range(4):
             queue = nc.sync if q % 2 == 0 else nc.scalar

@@ -50,17 +50,17 @@ def tile_rows_pl_mix_hyena_kernel(tc, x, w, dd, xs, x1, out_0, out_1, out_2):
         dd_cols = sb.tile([P, R], F32, name="dd_cols", align_bytes=64)
         dd_wide = sb.tile([P, N], F32, name="dd_wide", align_bytes=64)
         dd_all = sb.tile([P, N], F32, name="dd_all", align_bytes=64)
-        x_raw = [sb.tile([P, PACK, H], F32, name="x_raw%d" % h) for h in range(2)]
+        x_raw = sb.tile([P, PACK, N], F32, name="x_raw")
         x_bf = [sb.tile([P, H, PACK], BF16, name="x_bf%d" % h, align_bytes=64) for h in range(2)]
         x_codes = sb.tile([P, N], U32, name="x_codes", align_bytes=64)
         x_scales = sb.tile([P, N], U8, name="x_scales", align_bytes=64)
         xs_sb = [sb.tile([P, N], F32, name="xs%d" % g) for g in range(G)]
-        x1_sb = [sb.tile([P, G, H], F32, name="x1_%d" % h) for h in range(2)]
+        x1_sb = [sb.tile([P, 2, N], F32, name="x1_%d" % a) for a in range(2)]
         direct = [sb.tile([P, N], F32, name="direct%d" % g) for g in range(G)]
-        summed = sb.tile([P, G, N], F32, name="summed")
-        y = [sb.tile([P, G, H], F32, name="y%d" % h) for h in range(2)]
-        y_bf = [sb.tile([P, G, H], BF16, name="y_bf%d" % h) for h in range(2)]
-        y_moved = [sb.tile([P, PACK, H], BF16, name="y_moved%d" % h) for h in range(2)]
+        summed = [sb.tile([P, 2, N], F32, name="summed%d" % a) for a in range(2)]
+        y = [sb.tile([P, 2, N], F32, name="y%d" % a) for a in range(2)]
+        y_bf = [sb.tile([P, 2, N], BF16, name="y_bf%d" % a) for a in range(2)]
+        y_moved = sb.tile([P, PACK, N], BF16, name="y_moved")
         y_words = [sb.tile([P, H, PACK], BF16, name="y_words%d" % h, align_bytes=64) for h in range(2)]
         y_codes = sb.tile([P, N], U32, name="y_codes", align_bytes=64)
         y_scales = sb.tile([P, N], U8, name="y_scales", align_bytes=64)
@@ -83,25 +83,25 @@ def tile_rows_pl_mix_hyena_kernel(tc, x, w, dd, xs, x1, out_0, out_1, out_2):
         interleave(nc.scalar.copy, w_bf[:], w_raw[:])
         nc.vector.transpose(out=dd_cols[:], in_=dd_rows[:])
         quantize(w_codes[:R], w_scales[:R], w_bf[:], slice(0, M))
-        for h in range(2):
-            nc.sync.dma_start(out=x_raw[h][:], in_=x_rows[:, :, H * h : H * (h + 1)])
+        nc.sync.dma_start(out=x_raw[:], in_=x_rows)
         for g in range(1, G):
             nc.sync.dma_start(out=w_mx[R * g : R * (g + 1)], in_=w_mx[:R])
-        for g in range(G):
+        for g in range(3):
             nc.sync.dma_start(out=xs_sb[g][:], in_=xs[g])
-        for h in range(2):
-            nc.sync.dma_start(out=x1_sb[h][:], in_=x1_rows[:, :, H * h : H * (h + 1)])
+        nc.sync.dma_start(out=x1_sb[0][:], in_=x1_rows[:, 0:2, :])
+        nc.sync.dma_start(out=xs_sb[3][:], in_=xs[3])
+        nc.sync.dma_start(out=x1_sb[1][:], in_=x1_rows[:, 2:4, :])
 
-        interleave(nc.scalar.copy, x_bf[0][:], x_raw[0][:])
         nc.vector.tensor_copy(
             out=dd_wide[:].rearrange("p (b i) -> p b i", i=R),
             in_=dd_cols[:, 0:16].unsqueeze(2).to_broadcast([P, 16, R]),
         )
         nc.vector.transpose(out=dd_all[:], in_=dd_wide[:])
         split = 160
+        interleave(nc.scalar.copy, x_bf[1][:, :split, :], x_raw[:, :, H : H + split])
+        interleave(nc.vector.tensor_copy, x_bf[0][:], x_raw[:, :, :H])
+        interleave(nc.vector.tensor_copy, x_bf[1][:, split:, :], x_raw[:, :, H + split :])
         quantize(x_codes, x_scales, x_bf[0][:], slice(0, H))
-        interleave(nc.vector.tensor_copy, x_bf[1][:, :split, :], x_raw[1][:, :, :split])
-        interleave(nc.scalar.copy, x_bf[1][:, split:, :], x_raw[1][:, :, split:])
         quantize(x_codes, x_scales, x_bf[1][:], slice(H, N))
 
         for g in range(G):
@@ -120,18 +120,16 @@ def tile_rows_pl_mix_hyena_kernel(tc, x, w, dd, xs, x1, out_0, out_1, out_2):
             nc.vector.tensor_tensor(out=direct[g][:], in0=xs_sb[g][:], in1=dd_all[:], op=MULT)
 
         def add_direct(g):
-            nc.vector.tensor_tensor(out=summed[:, g, :], in0=z[g][:], in1=direct[g][:], op=ADD)
+            nc.vector.tensor_tensor(out=summed[g // 2][:, g % 2, :], in0=z[g][:], in1=direct[g][:], op=ADD)
 
-        def gate(out, h, groups):
-            nc.vector.tensor_tensor(
-                out=out[:, groups, :], in0=summed[:, groups, H * h : H * (h + 1)], in1=x1_sb[h][:, groups, :], op=MULT
-            )
+        def gate(out, in0, in1):
+            nc.vector.tensor_tensor(out=out, in0=in0, in1=in1, op=MULT)
 
-        def move(queue, h, g):
-            queue.dma_start(out=y_moved[h][R * g : R * (g + 1)], in_=y_bf[h][:, g, :])
+        def move(queue, g, cols):
+            queue.dma_start(out=y_moved[R * g : R * (g + 1), :, cols], in_=y_bf[g // 2][:, g % 2, cols])
 
-        def store_y(h):
-            nc.sync.dma_start(out=y_rows[:, :, H * h : H * (h + 1)], in_=y[h][:])
+        def store_y(a):
+            nc.sync.dma_start(out=y_rows[:, 2 * a : 2 * a + 2, :], in_=y[a][:])
 
         def planes(h):
             cols = slice(H * h, H * (h + 1))
@@ -141,26 +139,27 @@ def tile_rows_pl_mix_hyena_kernel(tc, x, w, dd, xs, x1, out_0, out_1, out_2):
         direct_term(0)
         direct_term(1)
         add_direct(0)
-        direct_term(2)
         add_direct(1)
+        direct_term(2)
+        for g in range(2):
+            gate(y[0][:, g, :], summed[0][:, g, :], x1_sb[0][:, g, :])
+            nc.scalar.copy(out=y_bf[0][:, g, :], in_=y[0][:, g, :])
+            move(nc.scalar, g, slice(0, N))
+        store_y(0)
         direct_term(3)
         add_direct(2)
         add_direct(3)
-        for g in (0, 2):
-            gate(y[0], 0, slice(g, g + 2))
-            nc.scalar.copy(out=y_bf[0][:, g : g + 2, :], in_=y[0][:, g : g + 2, :])
-            move(nc.sync, 0, g)
-            move(nc.sync, 0, g + 1)
-        for g, queue in ((0, nc.scalar), (2, nc.sync)):
-            gate(y_bf[1], 1, slice(g, g + 2))
-            move(queue, 1, g)
-            move(queue, 1, g + 1)
-        store_y(0)
-        gate(y[1], 1, slice(0, G))
+        for h in range(2):
+            cols = slice(H * h, H * (h + 1))
+            gate(y_bf[1][:, :, cols], summed[1][:, :, cols], x1_sb[1][:, :, cols])
+            move(nc.scalar, 2, cols)
+            move(nc.sync, 3, cols)
+        gate(y[1][:], summed[1][:], x1_sb[1][:])
         store_y(1)
         for h in range(2):
-            interleave(nc.vector.tensor_copy, y_words[h][:, :split, :], y_moved[h][:, :, :split])
-            interleave(nc.scalar.copy, y_words[h][:, split:, :], y_moved[h][:, :, split:])
+            lo, mid, hi = H * h, H * h + split, H * (h + 1)
+            interleave(nc.vector.tensor_copy, y_words[h][:, :split, :], y_moved[:, :, lo:mid])
+            interleave(nc.scalar.copy, y_words[h][:, split:, :], y_moved[:, :, mid:hi])
         planes(0)
         planes(1)
         for q in range(4):

@@ -18,6 +18,10 @@ P = 128
 R = 32
 PACK = 4
 H = N // 2
+X_HEAD = 384
+X_SCALAR = 160
+X_TAIL_VECTOR = 72
+Y_VECTOR = 144
 
 
 def interleave(engine_copy, dst, src):
@@ -34,7 +38,7 @@ def tile_rows_pl_mix_hyena_kernel(tc, x, w, dd, xs, x1, out_0, out_1, out_2):
     y_rows = out_0.rearrange("(g m) n -> m g n", g=G)
     x1_rows = x1.rearrange("g m n -> m g n")
     words_out = out_1.rearrange("v p n u -> (v p) (n u)").bitcast(I32)
-    scales_out = out_2.rearrange("v f n -> (v f) n").bitcast(I32)
+    scales_out = out_2.rearrange("v (a k f) n -> k (v a) f n", a=2, k=2).bitcast(I32)
 
     with ExitStack() as ctx:
         sb = ctx.enter_context(tc.tile_pool(name="sb", bufs=1))
@@ -50,8 +54,9 @@ def tile_rows_pl_mix_hyena_kernel(tc, x, w, dd, xs, x1, out_0, out_1, out_2):
         dd_cols = sb.tile([P, R], F32, name="dd_cols", align_bytes=64)
         dd_wide = sb.tile([P, N], F32, name="dd_wide", align_bytes=64)
         dd_all = sb.tile([P, N], F32, name="dd_all", align_bytes=64)
-        x_raw = sb.tile([P, PACK, N], F32, name="x_raw")
-        x_bf = [sb.tile([P, H, PACK], BF16, name="x_bf%d" % h, align_bytes=64) for h in range(2)]
+        x_head = sb.tile([P, PACK, X_HEAD], F32, name="x_head")
+        x_tail = sb.tile([P, PACK, N - X_HEAD], F32, name="x_tail")
+        x_bf = sb.tile([P, N, PACK], BF16, name="x_bf", align_bytes=64)
         x_codes = sb.tile([P, N], U32, name="x_codes", align_bytes=64)
         x_scales = sb.tile([P, N], U8, name="x_scales", align_bytes=64)
         xs_sb = [sb.tile([P, N], F32, name="xs%d" % g) for g in range(G)]
@@ -60,10 +65,10 @@ def tile_rows_pl_mix_hyena_kernel(tc, x, w, dd, xs, x1, out_0, out_1, out_2):
         summed = [sb.tile([P, 2, N], F32, name="summed%d" % a) for a in range(2)]
         y = [sb.tile([P, 2, N], F32, name="y%d" % a) for a in range(2)]
         y_bf = [sb.tile([P, 2, N], BF16, name="y_bf%d" % a) for a in range(2)]
-        y_moved = sb.tile([P, PACK, N], BF16, name="y_moved")
-        y_words = [sb.tile([P, H, PACK], BF16, name="y_words%d" % h, align_bytes=64) for h in range(2)]
-        y_codes = sb.tile([P, N], U32, name="y_codes", align_bytes=64)
-        y_scales = sb.tile([P, N], U8, name="y_scales", align_bytes=64)
+        y_moved = [sb.tile([P, PACK, H], BF16, name="y_moved%d" % a) for a in range(2)]
+        y_words = [sb.tile([P, H, PACK], BF16, name="y_words%d" % a, align_bytes=64) for a in range(2)]
+        y_codes = [sb.tile([P, H], U32, name="y_codes%d" % a, align_bytes=64) for a in range(2)]
+        y_scales = sb.tile([P, H], U8, name="y_scales", align_bytes=64)
         z = [ps.tile([P, N], F32, name="z%d" % g) for g in range(G)]
 
         nc.sync.dma_start(out=w_raw[:], in_=w_rows)
@@ -80,29 +85,34 @@ def tile_rows_pl_mix_hyena_kernel(tc, x, w, dd, xs, x1, out_0, out_1, out_2):
             )
 
         nc.vector.memset(w_mx[:R, M:], 0)
-        interleave(nc.scalar.copy, w_bf[:], w_raw[:])
         nc.vector.transpose(out=dd_cols[:], in_=dd_rows[:])
-        quantize(w_codes[:R], w_scales[:R], w_bf[:], slice(0, M))
-        nc.sync.dma_start(out=x_raw[:], in_=x_rows)
-        for g in range(1, G):
-            nc.sync.dma_start(out=w_mx[R * g : R * (g + 1)], in_=w_mx[:R])
-        for g in range(3):
-            nc.sync.dma_start(out=xs_sb[g][:], in_=xs[g])
-        nc.sync.dma_start(out=x1_sb[0][:], in_=x1_rows[:, 0:2, :])
-        nc.sync.dma_start(out=xs_sb[3][:], in_=xs[3])
-        nc.sync.dma_start(out=x1_sb[1][:], in_=x1_rows[:, 2:4, :])
-
-        nc.vector.tensor_copy(
+        interleave(nc.vector.tensor_copy, w_bf[:], w_raw[:])
+        nc.scalar.copy(
             out=dd_wide[:].rearrange("p (b i) -> p b i", i=R),
             in_=dd_cols[:, 0:16].unsqueeze(2).to_broadcast([P, 16, R]),
         )
+        quantize(w_codes[:R], w_scales[:R], w_bf[:], slice(0, M))
+        nc.sync.dma_start(out=x_head[:], in_=x_rows[:, :, :X_HEAD])
+        nc.sync.dma_start(out=x_tail[:], in_=x_rows[:, :, X_HEAD:])
+        nc.sync.dma_start(out=xs_sb[0][:], in_=xs[0])
+        for g in range(1, G):
+            nc.sync.dma_start(out=w_mx[R * g : R * (g + 1)], in_=w_mx[:R])
+        nc.sync.dma_start(out=xs_sb[1][:], in_=xs[1])
+        nc.sync.dma_start(out=x1_sb[0][:], in_=x1_rows[:, 0:2, :])
+        for g in range(2, G):
+            nc.sync.dma_start(out=xs_sb[g][:], in_=xs[g])
+        nc.sync.dma_start(out=x1_sb[1][:], in_=x1_rows[:, 2:4, :])
+
         nc.vector.transpose(out=dd_all[:], in_=dd_wide[:])
-        split = 160
-        interleave(nc.scalar.copy, x_bf[1][:, :split, :], x_raw[:, :, H : H + split])
-        interleave(nc.vector.tensor_copy, x_bf[0][:], x_raw[:, :, :H])
-        interleave(nc.vector.tensor_copy, x_bf[1][:, split:, :], x_raw[:, :, H + split :])
-        quantize(x_codes, x_scales, x_bf[0][:], slice(0, H))
-        quantize(x_codes, x_scales, x_bf[1][:], slice(H, N))
+        interleave(nc.scalar.copy, x_bf[:, :X_SCALAR, :], x_head[:, :, :X_SCALAR])
+        interleave(nc.vector.tensor_copy, x_bf[:, H:X_HEAD, :], x_head[:, :, H:])
+        interleave(nc.vector.tensor_copy, x_bf[:, X_SCALAR:H, :], x_head[:, :, X_SCALAR:H])
+        quantize(x_codes, x_scales, x_bf[:, H:X_HEAD, :], slice(H, X_HEAD))
+        cut = X_HEAD + X_TAIL_VECTOR
+        interleave(nc.vector.tensor_copy, x_bf[:, X_HEAD:cut, :], x_tail[:, :, :X_TAIL_VECTOR])
+        interleave(nc.scalar.copy, x_bf[:, cut:, :], x_tail[:, :, X_TAIL_VECTOR:])
+        quantize(x_codes, x_scales, x_bf[:, :H, :], slice(0, H))
+        quantize(x_codes, x_scales, x_bf[:, X_HEAD:, :], slice(X_HEAD, N))
 
         for g in range(G):
             rows = slice(R * g, R * (g + 1))
@@ -125,43 +135,52 @@ def tile_rows_pl_mix_hyena_kernel(tc, x, w, dd, xs, x1, out_0, out_1, out_2):
         def gate(out, in0, in1):
             nc.vector.tensor_tensor(out=out, in0=in0, in1=in1, op=MULT)
 
-        def move(queue, g, cols):
-            queue.dma_start(out=y_moved[R * g : R * (g + 1), :, cols], in_=y_bf[g // 2][:, g % 2, cols])
+        def move(queue, g, h):
+            first = 2 * R * h + R * (g % 2)
+            queue.dma_start(out=y_moved[g // 2][first : first + R], in_=y_bf[g // 2][:, g % 2, H * h : H * (h + 1)])
 
         def store_y(a):
             nc.sync.dma_start(out=y_rows[:, 2 * a : 2 * a + 2, :], in_=y[a][:])
 
-        def planes(h):
-            cols = slice(H * h, H * (h + 1))
-            quantize(y_codes, y_scales, y_words[h][:], cols)
-            nc.sync.dma_start(out=words_out[:, cols], in_=y_codes[:, cols].bitcast(I32))
+        def planes(a, queues):
+            quantize(y_codes[a], y_scales[4 * a :], y_words[a][:], slice(0, H))
+            for h in range(2):
+                queues[h].dma_start(
+                    out=words_out[2 * R * a : 2 * R * (a + 1), H * h : H * (h + 1)],
+                    in_=y_codes[a][2 * R * h : 2 * R * (h + 1), :].bitcast(I32),
+                )
 
         direct_term(0)
         direct_term(1)
         add_direct(0)
         add_direct(1)
-        direct_term(2)
         for g in range(2):
             gate(y[0][:, g, :], summed[0][:, g, :], x1_sb[0][:, g, :])
             nc.scalar.copy(out=y_bf[0][:, g, :], in_=y[0][:, g, :])
-            move(nc.scalar, g, slice(0, N))
+            move(nc.sync, g, 0)
+            move(nc.sync, g, 1)
         store_y(0)
+        interleave(nc.scalar.copy, y_words[0][:], y_moved[0][:])
+        direct_term(2)
         direct_term(3)
         add_direct(2)
         add_direct(3)
-        for h in range(2):
-            cols = slice(H * h, H * (h + 1))
-            gate(y_bf[1][:, :, cols], summed[1][:, :, cols], x1_sb[1][:, :, cols])
-            move(nc.scalar, 2, cols)
-            move(nc.sync, 3, cols)
+        gate(y_bf[1][:, 0, :], summed[1][:, 0, :], x1_sb[1][:, 0, :])
+        move(nc.sync, 2, 0)
+        move(nc.sync, 2, 1)
+        gate(y_bf[1][:, 1, :], summed[1][:, 1, :], x1_sb[1][:, 1, :])
+        move(nc.sync, 3, 0)
+        move(nc.scalar, 3, 1)
         gate(y[1][:], summed[1][:], x1_sb[1][:])
         store_y(1)
-        for h in range(2):
-            lo, mid, hi = H * h, H * h + split, H * (h + 1)
-            interleave(nc.vector.tensor_copy, y_words[h][:, :split, :], y_moved[:, :, lo:mid])
-            interleave(nc.scalar.copy, y_words[h][:, split:, :], y_moved[:, :, mid:hi])
-        planes(0)
-        planes(1)
+        planes(0, (nc.sync, nc.sync))
+        interleave(nc.vector.tensor_copy, y_words[1][:, :Y_VECTOR, :], y_moved[1][:, :, :Y_VECTOR])
+        interleave(nc.scalar.copy, y_words[1][:, Y_VECTOR:, :], y_moved[1][:, :, Y_VECTOR:])
+        planes(1, (nc.sync, nc.scalar))
         for q in range(4):
-            queue = nc.sync if q % 2 == 0 else nc.scalar
-            queue.dma_start(out=scales_out[4 * q : 4 * q + 4, :], in_=y_scales[R * q : R * q + 4, :].bitcast(I32))
+            h, k = q // 2, q % 2
+            queue = nc.sync if k == 0 else nc.scalar
+            queue.dma_start(
+                out=scales_out[k, :, :, H // 4 * h : H // 4 * (h + 1)],
+                in_=y_scales[R * q : R * q + 8, :].bitcast(I32),
+            )

@@ -8,7 +8,6 @@ FLOPS = 2 * G * D * M * N
 F32 = mybir.dt.float32
 BF16 = mybir.dt.bfloat16
 I32 = mybir.dt.int32
-U32 = mybir.dt.uint32
 U8 = mybir.dt.uint8
 FP8X4 = mybir.dt.float8_e4m3fn_x4
 ADD = mybir.AluOpType.add
@@ -17,11 +16,12 @@ MULT = mybir.AluOpType.mult
 P = 128
 R = 32
 PACK = 4
-H = N // 2
-X_HEAD = 384
-X_SCALAR = 160
-X_TAIL_VECTOR = 72
-Y_VECTOR = 144
+C = 128
+A = 3 * C
+A1 = 2 * C
+X_SCALAR = 144
+Y_VECTOR = 80
+PAD = M - R
 
 
 def interleave(engine_copy, dst, src):
@@ -35,152 +35,191 @@ def tile_rows_pl_mix_hyena_kernel(tc, x, w, dd, xs, x1, out_0, out_1, out_2):
     nc = tc.nc
     x_rows = x.rearrange("g (p j) n -> (g p) j n", j=PACK)
     w_rows = w.rearrange("(p j) m -> p j m", j=PACK)
-    y_rows = out_0.rearrange("(g m) n -> m g n", g=G)
-    x1_rows = x1.rearrange("g m n -> m g n")
+    xs_plain = xs.rearrange("g m n -> m g n")
+    x1_plain = x1.rearrange("g m n -> m g n")
+    y_plain = out_0.rearrange("(g m) n -> m g n", g=G)
+    xs_packed = xs.rearrange("g (p u) n -> (g p) u n", u=PACK)
+    x1_packed = x1.rearrange("g (p u) n -> (g p) u n", u=PACK)
+    y_packed = out_0.rearrange("(p u) n -> p u n", u=PACK)
     words_out = out_1.rearrange("v p n u -> (v p) (n u)").bitcast(I32)
-    scales_out = out_2.rearrange("v (a k f) n -> k (v a) f n", a=2, k=2).bitcast(I32)
+    scales_out = out_2.rearrange("v f n -> (v f) n").bitcast(I32)
 
     with ExitStack() as ctx:
         sb = ctx.enter_context(tc.tile_pool(name="sb", bufs=1))
         ps = ctx.enter_context(tc.psum_pool(name="ps", bufs=1))
         ctx.enter_context(tc.manual_schedule())
 
-        w_raw = sb.tile([R, PACK, M], F32, name="w_raw")
-        w_bf = sb.tile([R, M, PACK], BF16, name="w_bf", align_bytes=64)
-        w_mx = sb.tile([P, M + M // 4], I32, name="w_mx", align_bytes=64)
-        w_codes = w_mx[:, :M]
-        w_scales = w_mx[:, M:].bitcast(U8)
-        dd_rows = sb.tile([P, R], F32, name="dd_rows", align_bytes=64)
-        dd_cols = sb.tile([P, R], F32, name="dd_cols", align_bytes=64)
-        dd_wide = sb.tile([P, N], F32, name="dd_wide", align_bytes=64)
-        dd_all = sb.tile([P, N], F32, name="dd_all", align_bytes=64)
-        x_head = sb.tile([P, PACK, X_HEAD], F32, name="x_head")
-        x_tail = sb.tile([P, PACK, N - X_HEAD], F32, name="x_tail")
-        x_bf = sb.tile([P, N, PACK], BF16, name="x_bf", align_bytes=64)
-        x_codes = sb.tile([P, N], U32, name="x_codes", align_bytes=64)
-        x_scales = sb.tile([P, N], U8, name="x_scales", align_bytes=64)
-        xs_sb = [sb.tile([P, N], F32, name="xs%d" % g) for g in range(G)]
-        x1_sb = [sb.tile([P, 2, N], F32, name="x1_%d" % a) for a in range(2)]
-        direct = [sb.tile([P, N], F32, name="direct%d" % g) for g in range(G)]
-        summed = [sb.tile([P, 2, N], F32, name="summed%d" % a) for a in range(2)]
-        y = [sb.tile([P, 2, N], F32, name="y%d" % a) for a in range(2)]
-        y_bf = [sb.tile([P, 2, N], BF16, name="y_bf%d" % a) for a in range(2)]
-        y_moved = [sb.tile([P, PACK, H], BF16, name="y_moved%d" % a) for a in range(2)]
-        y_words = [sb.tile([P, H, PACK], BF16, name="y_words%d" % a, align_bytes=64) for a in range(2)]
-        y_codes = [sb.tile([P, H], U32, name="y_codes%d" % a, align_bytes=64) for a in range(2)]
-        y_scales = sb.tile([P, H], U8, name="y_scales", align_bytes=64)
+        def tile(name, shape, dtype):
+            return sb.tile(shape, dtype, name=name, align_bytes=64)
+
+        w_raw = tile("w_raw", [R, PACK, M], F32)
+        w_bf = tile("w_bf", [R, M, PACK], BF16)
+        w_mx = tile("w_mx", [P, M + M // 4], I32)
+        wd_bf = tile("wd_bf", [R, M, PACK], BF16)
+        wd_codes = tile("wd_codes", [R, M], I32)
+        wd_scales = tile("wd_scales", [R, M // 4], I32)
+        wz_codes = tile("wz_codes", [R, PAD + PACK * M], I32)
+        wz_scales = tile("wz_scales", [R, 96], I32)
+        dd_rows = tile("dd_rows", [P, R], F32)
+        dd_cols = tile("dd_cols", [P, R], F32)
+        dd_wide = tile("dd_wide", [P, N], F32)
+        dd_all = tile("dd_all", [P, N], F32)
+        xa_raw = tile("xa_raw", [P, PACK, A], F32)
+        xb_raw = tile("xb_raw", [P, PACK, C], F32)
+        xa_bf = tile("xa_bf", [P, A, PACK], BF16)
+        xb_bf = tile("xb_bf", [P, C, PACK], BF16)
+        xa_codes = tile("xa_codes", [P, A], I32)
+        xa_scales = tile("xa_scales", [P, A], U8)
+        xb_mx = tile("xb_mx", [P, C + C // 4], I32)
+        xb_copy = [xb_mx] + [tile("xb_copy%d" % g, [R, C + C // 4], I32) for g in range(1, G)]
+        xs_a = [tile("xs_a%d" % a, [P, 2, A], F32) for a in range(2)]
+        x1_a = tile("x1_a", [P, G, A], F32)
+        xs_b = tile("xs_b", [P, PACK, C], F32)
+        x1_b = tile("x1_b", [P, PACK, C], F32)
+        widths = (A1, C)
+        starts = (0, A1)
+        direct = [tile("direct%d" % k, [P, G, widths[k]], F32) for k in range(2)]
+        summed = [tile("summed%d" % k, [P, G, widths[k]], F32) for k in range(2)]
+        y = [tile("y%d" % k, [P, G, widths[k]], F32) for k in range(2)]
+        y_bf = [[tile("y_bf%d_%d" % (k, g), [P, widths[k]], BF16) for g in range(G)] for k in range(2)]
+        y_moved = [tile("y_moved%d" % k, [P, PACK, widths[k]], BF16) for k in range(2)]
+        direct_b = tile("direct_b", [P, PACK, C], F32)
+        summed_b = tile("summed_b", [P, PACK, C], F32)
+        y_b = tile("y_b", [P, PACK, C], F32)
+        y_words = [tile("y_words%d" % h, [P, A1, PACK], BF16) for h in range(2)]
+        y_codes = [tile("y_codes%d" % h, [P, A1], I32) for h in range(2)]
+        y_scales = tile("y_scales", [P, N], U8)
         z = [ps.tile([P, N], F32, name="z%d" % g) for g in range(G)]
+        z_b = ps.tile([P, N], F32, name="z_b")
+
+        def quantize(codes, scales, src):
+            nc.vector.quantize_mx(out=codes.bitcast(FP8X4), scales=scales, in_=src.rearrange("p c j -> p (c j)"))
+
+        def product(out, w_c, w_s, x_c, x_s, start, stop):
+            nc.tensor.matmul_mx(
+                out=out, lhsT=w_c.bitcast(FP8X4), lhsT_scale=w_s, rhs=x_c.bitcast(FP8X4), rhs_scale=x_s,
+                start=start, stop=stop,
+            )
+
+        def binary(op, out, in0, in1):
+            nc.vector.tensor_tensor(out=out, in0=in0, in1=in1, op=op)
 
         nc.sync.dma_start(out=w_raw[:], in_=w_rows)
         nc.scalar.dma_start(
             out=dd_rows[:],
             in_=dd.rearrange("o (b i) -> o b i", i=R).broadcast_to([P // 16, 16, R]),
         )
-
-        def quantize(codes, scales, src, cols):
-            nc.vector.quantize_mx(
-                out=codes[:, cols].bitcast(FP8X4),
-                scales=scales[:, cols],
-                in_=src.rearrange("p c j -> p (c j)"),
-            )
+        nc.sync.dma_start(out=xa_raw[:], in_=x_rows[:, :, :A])
+        nc.sync.dma_start(out=xs_a[0][:], in_=xs_plain[:, 0:2, :A])
+        nc.sync.dma_start(out=xb_raw[:], in_=x_rows[:, :, A:])
+        nc.sync.dma_start(out=xs_a[1][:], in_=xs_plain[:, 2:4, :A])
 
         nc.vector.memset(w_mx[:R, M:], 0)
+        nc.vector.memset(xb_mx[:, C:], 0)
+        nc.vector.memset(wz_codes[:], 0)
+        nc.vector.memset(wz_scales[:], 0)
+        nc.vector.memset(wd_scales[:], 0)
         nc.vector.transpose(out=dd_cols[:], in_=dd_rows[:])
         interleave(nc.vector.tensor_copy, w_bf[:], w_raw[:])
         nc.scalar.copy(
             out=dd_wide[:].rearrange("p (b i) -> p b i", i=R),
             in_=dd_cols[:, 0:16].unsqueeze(2).to_broadcast([P, 16, R]),
         )
-        quantize(w_codes[:R], w_scales[:R], w_bf[:], slice(0, M))
-        nc.sync.dma_start(out=x_head[:], in_=x_rows[:, :, :X_HEAD])
-        nc.sync.dma_start(out=x_tail[:], in_=x_rows[:, :, X_HEAD:])
-        nc.sync.dma_start(out=xs_sb[0][:], in_=xs[0])
+        quantize(w_mx[:R, :M], w_mx[:R, M:].bitcast(U8), w_bf[:])
         for g in range(1, G):
-            nc.sync.dma_start(out=w_mx[R * g : R * (g + 1)], in_=w_mx[:R])
-        nc.sync.dma_start(out=xs_sb[1][:], in_=xs[1])
-        nc.sync.dma_start(out=x1_sb[0][:], in_=x1_rows[:, 0:2, :])
-        for g in range(2, G):
-            nc.sync.dma_start(out=xs_sb[g][:], in_=xs[g])
-        nc.sync.dma_start(out=x1_sb[1][:], in_=x1_rows[:, 2:4, :])
+            queue = nc.scalar if g == 1 else nc.sync
+            queue.dma_start(out=w_mx[R * g : R * (g + 1)], in_=w_mx[:R])
+        nc.sync.dma_start(out=x1_a[:], in_=x1_plain[:, :, :A])
 
         nc.vector.transpose(out=dd_all[:], in_=dd_wide[:])
-        interleave(nc.scalar.copy, x_bf[:, :X_SCALAR, :], x_head[:, :, :X_SCALAR])
-        interleave(nc.vector.tensor_copy, x_bf[:, H:X_HEAD, :], x_head[:, :, H:])
-        interleave(nc.vector.tensor_copy, x_bf[:, X_SCALAR:H, :], x_head[:, :, X_SCALAR:H])
-        quantize(x_codes, x_scales, x_bf[:, H:X_HEAD, :], slice(H, X_HEAD))
-        cut = X_HEAD + X_TAIL_VECTOR
-        interleave(nc.vector.tensor_copy, x_bf[:, X_HEAD:cut, :], x_tail[:, :, :X_TAIL_VECTOR])
-        interleave(nc.scalar.copy, x_bf[:, cut:, :], x_tail[:, :, X_TAIL_VECTOR:])
-        quantize(x_codes, x_scales, x_bf[:, :H, :], slice(0, H))
-        quantize(x_codes, x_scales, x_bf[:, X_HEAD:, :], slice(X_HEAD, N))
+        interleave(nc.scalar.copy, xa_bf[:, :X_SCALAR, :], xa_raw[:, :, :X_SCALAR])
+        interleave(nc.vector.tensor_copy, xa_bf[:, A1:, :], xa_raw[:, :, A1:])
+        interleave(nc.vector.tensor_copy, xa_bf[:, X_SCALAR:A1, :], xa_raw[:, :, X_SCALAR:A1])
+        quantize(xa_codes[:, A1:], xa_scales[:, A1:], xa_bf[:, A1:, :])
+        quantize(xa_codes[:, :A1], xa_scales[:, :A1], xa_bf[:, :A1, :])
+        interleave(nc.scalar.copy, xb_bf[:], xb_raw[:])
+        nc.scalar.copy(
+            out=wd_bf[:].rearrange("p (u i) j -> p u i j", u=PACK),
+            in_=w_raw[:].rearrange("p j (i u) -> p u i j", u=PACK),
+        )
 
         for g in range(G):
             rows = slice(R * g, R * (g + 1))
-            nc.tensor.matmul_mx(
-                out=z[g][:],
-                lhsT=w_codes[rows, :].bitcast(FP8X4),
-                lhsT_scale=w_scales[rows, :],
-                rhs=x_codes[rows, :].bitcast(FP8X4),
-                rhs_scale=x_scales[rows, :],
-                start=True,
-                stop=True,
-            )
+            for c in range(A // C):
+                cols = slice(C * c, C * (c + 1))
+                product(z[g][:, cols], w_mx[rows, :M], w_mx[rows, M:].bitcast(U8),
+                        xa_codes[rows, cols], xa_scales[rows, cols], True, True)
 
-        def direct_term(g):
-            nc.vector.tensor_tensor(out=direct[g][:], in0=xs_sb[g][:], in1=dd_all[:], op=MULT)
+        def direct_term(k, a):
+            cols = slice(starts[k], starts[k] + widths[k])
+            binary(MULT, direct[k][:, 2 * a : 2 * a + 2, :], xs_a[a][:, :, cols],
+                   dd_all[:, cols].unsqueeze(1).to_broadcast([P, 2, widths[k]]))
 
-        def add_direct(g):
-            nc.vector.tensor_tensor(out=summed[g // 2][:, g % 2, :], in0=z[g][:], in1=direct[g][:], op=ADD)
+        def add_direct(k, g):
+            binary(ADD, summed[k][:, g, :], z[g][:, starts[k] : starts[k] + widths[k]], direct[k][:, g, :])
 
-        def gate(out, in0, in1):
-            nc.vector.tensor_tensor(out=out, in0=in0, in1=in1, op=MULT)
+        def gate_round_move(k, g):
+            binary(MULT, y[k][:, g, :], summed[k][:, g, :], x1_a[:, g, starts[k] : starts[k] + widths[k]])
+            nc.scalar.copy(out=y_bf[k][g][:], in_=y[k][:, g, :])
+            nc.sync.dma_start(out=y_moved[k][R * g : R * (g + 1)], in_=y_bf[k][g][:])
 
-        def move(queue, g, h):
-            first = 2 * R * h + R * (g % 2)
-            queue.dma_start(out=y_moved[g // 2][first : first + R], in_=y_bf[g // 2][:, g % 2, H * h : H * (h + 1)])
+        direct_term(0, 0)
+        quantize(xb_mx[:, :C], xb_mx[:, C:].bitcast(U8), xb_bf[:])
+        for g in range(1, G):
+            nc.sync.dma_start(out=xb_copy[g][:], in_=xb_mx[R * g : R * (g + 1)])
+        nc.sync.dma_start(out=xs_b[:], in_=xs_packed[:, :, A:])
+        nc.sync.dma_start(out=x1_b[:], in_=x1_packed[:, :, A:])
+        direct_term(0, 1)
+        add_direct(0, 0)
+        quantize(wd_codes[:], wd_scales[:].bitcast(U8), wd_bf[:])
+        add_direct(0, 1)
+        nc.vector.tensor_copy(
+            out=wz_codes[:, PAD:].rearrange("p (u m) -> p u m", u=PACK)[:, :, :R],
+            in_=wd_codes[:].rearrange("p (u i) -> p u i", u=PACK),
+        )
+        nc.vector.tensor_copy(
+            out=wz_scales[:, 16:80].rearrange("p (u r i) -> p u r i", u=PACK, r=2),
+            in_=wd_scales[:].rearrange("p (u i) -> p u i", u=PACK).unsqueeze(2).to_broadcast([R, PACK, 2, 8]),
+        )
+        for u in range(PACK):
+            for g in range(G):
+                first = PAD + M * u - R * g
+                first_scale = 16 + 16 * u - 16 * (g // 2)
+                product(z_b[:, C * u : C * (u + 1)], wz_codes[:, first : first + M],
+                        wz_scales[:, first_scale : first_scale + M // 4].bitcast(U8),
+                        xb_copy[g][:R, :C], xb_copy[g][:R, C:].bitcast(U8), g == 0, g == G - 1)
 
-        def store_y(a):
-            nc.sync.dma_start(out=y_rows[:, 2 * a : 2 * a + 2, :], in_=y[a][:])
-
-        def planes(a, queues):
-            quantize(y_codes[a], y_scales[4 * a :], y_words[a][:], slice(0, H))
-            for h in range(2):
-                queues[h].dma_start(
-                    out=words_out[2 * R * a : 2 * R * (a + 1), H * h : H * (h + 1)],
-                    in_=y_codes[a][2 * R * h : 2 * R * (h + 1), :].bitcast(I32),
-                )
-
-        direct_term(0)
-        direct_term(1)
-        add_direct(0)
-        add_direct(1)
-        for g in range(2):
-            gate(y[0][:, g, :], summed[0][:, g, :], x1_sb[0][:, g, :])
-            nc.scalar.copy(out=y_bf[0][:, g, :], in_=y[0][:, g, :])
-            move(nc.sync, g, 0)
-            move(nc.sync, g, 1)
-        store_y(0)
+        for g in range(2, G):
+            add_direct(0, g)
+        for g in range(G):
+            gate_round_move(0, g)
+        nc.sync.dma_start(out=y_plain[:, :, :A1], in_=y[0][:])
+        for a in range(2):
+            direct_term(1, a)
+        for g in range(G):
+            add_direct(1, g)
+        for g in range(G):
+            gate_round_move(1, g)
+        nc.sync.dma_start(out=y_plain[:, :, A1:A], in_=y[1][:])
         interleave(nc.scalar.copy, y_words[0][:], y_moved[0][:])
-        direct_term(2)
-        direct_term(3)
-        add_direct(2)
-        add_direct(3)
-        gate(y_bf[1][:, 0, :], summed[1][:, 0, :], x1_sb[1][:, 0, :])
-        move(nc.sync, 2, 0)
-        move(nc.sync, 2, 1)
-        gate(y_bf[1][:, 1, :], summed[1][:, 1, :], x1_sb[1][:, 1, :])
-        move(nc.sync, 3, 0)
-        move(nc.scalar, 3, 1)
-        gate(y[1][:], summed[1][:], x1_sb[1][:])
-        store_y(1)
-        planes(0, (nc.sync, nc.sync))
+
+        halves = (slice(0, 2), slice(2, 4))
+        z_b_places = z_b[:].rearrange("p (u n) -> p u n", u=PACK)
+        for us in halves:
+            binary(MULT, direct_b[:, us, :], xs_b[:, us, :], dd_all[:, A:].unsqueeze(1).to_broadcast([P, 2, C]))
+        for us in halves:
+            binary(ADD, summed_b[:, us, :], z_b_places[:, us, :], direct_b[:, us, :])
+        for us in halves:
+            binary(MULT, y_b[:, us, :], summed_b[:, us, :], x1_b[:, us, :])
+        nc.sync.dma_start(out=y_packed[:, :, A:], in_=y_b[:])
+        quantize(y_codes[0][:], y_scales[:, :A1], y_words[0][:])
+        nc.sync.dma_start(out=words_out[:, :A1], in_=y_codes[0][:])
+        interleave(nc.vector.tensor_copy, y_words[1][:, C:, :], y_b[:])
+        interleave(nc.scalar.copy, y_words[1][:, Y_VECTOR:C, :], y_moved[1][:, :, Y_VECTOR:])
         interleave(nc.vector.tensor_copy, y_words[1][:, :Y_VECTOR, :], y_moved[1][:, :, :Y_VECTOR])
-        interleave(nc.scalar.copy, y_words[1][:, Y_VECTOR:, :], y_moved[1][:, :, Y_VECTOR:])
-        planes(1, (nc.sync, nc.scalar))
-        for q in range(4):
-            h, k = q // 2, q % 2
-            queue = nc.sync if k == 0 else nc.scalar
-            queue.dma_start(
-                out=scales_out[k, :, :, H // 4 * h : H // 4 * (h + 1)],
-                in_=y_scales[R * q : R * q + 8, :].bitcast(I32),
-            )
+        quantize(y_codes[1][:, C:], y_scales[:, A:], y_words[1][:, C:, :])
+        quantize(y_codes[1][:, :C], y_scales[:, A1:A], y_words[1][:, :C, :])
+        nc.sync.dma_start(out=words_out[:, A1:], in_=y_codes[1][:])
+        for q in range(G):
+            queue = nc.scalar if q % 2 == 0 else nc.sync
+            queue.dma_start(out=scales_out[4 * q : 4 * q + 4, :], in_=y_scales[R * q : R * q + 4, :].bitcast(I32))

@@ -19,7 +19,7 @@ PACK = 4
 C = 128
 A = 3 * C
 A1 = 2 * C
-X_SCALAR = 144
+X_SCALAR = 128
 Y_VECTOR = 80
 PAD = M - R
 
@@ -64,8 +64,7 @@ def tile_rows_pl_mix_hyena_kernel(tc, x, w, dd, xs, x1, out_0, out_1, out_2):
         dd_cols = tile("dd_cols", [P, R], F32)
         dd_wide = tile("dd_wide", [P, N], F32)
         dd_all = tile("dd_all", [P, N], F32)
-        xa_raw = tile("xa_raw", [P, PACK, A], F32)
-        xb_raw = tile("xb_raw", [P, PACK, C], F32)
+        x_raw = tile("x_raw", [P, PACK, N], F32)
         xa_bf = tile("xa_bf", [P, A, PACK], BF16)
         xb_bf = tile("xb_bf", [P, C, PACK], BF16)
         xa_codes = tile("xa_codes", [P, A], I32)
@@ -73,7 +72,7 @@ def tile_rows_pl_mix_hyena_kernel(tc, x, w, dd, xs, x1, out_0, out_1, out_2):
         xb_mx = tile("xb_mx", [P, C + C // 4], I32)
         xb_copy = [xb_mx] + [tile("xb_copy%d" % g, [R, C + C // 4], I32) for g in range(1, G)]
         xs_a = [tile("xs_a%d" % a, [P, 2, A], F32) for a in range(2)]
-        x1_a = tile("x1_a", [P, G, A], F32)
+        x1_a = [tile("x1_a%d" % a, [P, 2, A], F32) for a in range(2)]
         xs_b = tile("xs_b", [P, PACK, C], F32)
         x1_b = tile("x1_b", [P, PACK, C], F32)
         widths = (A1, C)
@@ -109,10 +108,9 @@ def tile_rows_pl_mix_hyena_kernel(tc, x, w, dd, xs, x1, out_0, out_1, out_2):
             out=dd_rows[:],
             in_=dd.rearrange("o (b i) -> o b i", i=R).broadcast_to([P // 16, 16, R]),
         )
-        nc.sync.dma_start(out=xa_raw[:], in_=x_rows[:, :, :A])
-        nc.sync.dma_start(out=xs_a[0][:], in_=xs_plain[:, 0:2, :A])
-        nc.sync.dma_start(out=xb_raw[:], in_=x_rows[:, :, A:])
-        nc.sync.dma_start(out=xs_a[1][:], in_=xs_plain[:, 2:4, :A])
+        nc.sync.dma_start(out=x_raw[:], in_=x_rows)
+        for a in range(2):
+            nc.sync.dma_start(out=xs_a[a][:], in_=xs_plain[:, 2 * a : 2 * a + 2, :A])
 
         nc.vector.memset(w_mx[:R, M:], 0)
         nc.vector.memset(xb_mx[:, C:], 0)
@@ -120,32 +118,41 @@ def tile_rows_pl_mix_hyena_kernel(tc, x, w, dd, xs, x1, out_0, out_1, out_2):
         nc.vector.memset(wz_scales[:], 0)
         nc.vector.memset(wd_scales[:], 0)
         nc.vector.transpose(out=dd_cols[:], in_=dd_rows[:])
-        interleave(nc.vector.tensor_copy, w_bf[:], w_raw[:])
-        nc.scalar.copy(
+        interleave(nc.scalar.copy, w_bf[:], w_raw[:])
+        nc.vector.tensor_copy(
             out=dd_wide[:].rearrange("p (b i) -> p b i", i=R),
             in_=dd_cols[:, 0:16].unsqueeze(2).to_broadcast([P, 16, R]),
         )
-        quantize(w_mx[:R, :M], w_mx[:R, M:].bitcast(U8), w_bf[:])
-        for g in range(1, G):
-            queue = nc.scalar if g == 1 else nc.sync
-            queue.dma_start(out=w_mx[R * g : R * (g + 1)], in_=w_mx[:R])
-        nc.sync.dma_start(out=x1_a[:], in_=x1_plain[:, :, :A])
-
-        nc.vector.transpose(out=dd_all[:], in_=dd_wide[:])
-        interleave(nc.scalar.copy, xa_bf[:, :X_SCALAR, :], xa_raw[:, :, :X_SCALAR])
-        interleave(nc.vector.tensor_copy, xa_bf[:, A1:, :], xa_raw[:, :, A1:])
-        interleave(nc.vector.tensor_copy, xa_bf[:, X_SCALAR:A1, :], xa_raw[:, :, X_SCALAR:A1])
-        quantize(xa_codes[:, A1:], xa_scales[:, A1:], xa_bf[:, A1:, :])
-        quantize(xa_codes[:, :A1], xa_scales[:, :A1], xa_bf[:, :A1, :])
-        interleave(nc.scalar.copy, xb_bf[:], xb_raw[:])
         nc.scalar.copy(
             out=wd_bf[:].rearrange("p (u i) j -> p u i j", u=PACK),
             in_=w_raw[:].rearrange("p j (i u) -> p u i j", u=PACK),
         )
+        nc.vector.transpose(out=dd_all[:], in_=dd_wide[:])
+        quantize(w_mx[:R, :M], w_mx[:R, M:].bitcast(U8), w_bf[:])
+        for g in range(1, G):
+            queue = nc.scalar if g == 1 else nc.sync
+            queue.dma_start(out=w_mx[R * g : R * (g + 1)], in_=w_mx[:R])
+        for a in range(2):
+            nc.sync.dma_start(out=x1_a[a][:], in_=x1_plain[:, 2 * a : 2 * a + 2, :A])
+        quantize(wd_codes[:], wd_scales[:].bitcast(U8), wd_bf[:])
+
+        interleave(nc.scalar.copy, xa_bf[:, :X_SCALAR, :], x_raw[:, :, :X_SCALAR])
+        interleave(nc.vector.tensor_copy, xa_bf[:, X_SCALAR:, :], x_raw[:, :, X_SCALAR:A])
+        nc.vector.tensor_copy(
+            out=wz_codes[:, PAD:].rearrange("p (u m) -> p u m", u=PACK)[:, :, :R],
+            in_=wd_codes[:].rearrange("p (u i) -> p u i", u=PACK),
+        )
+        nc.vector.tensor_copy(
+            out=wz_scales[:, 16:80].rearrange("p (u r i) -> p u r i", u=PACK, r=2),
+            in_=wd_scales[:].rearrange("p (u i) -> p u i", u=PACK).unsqueeze(2).to_broadcast([R, PACK, 2, 8]),
+        )
+        quantize(xa_codes[:, C:], xa_scales[:, C:], xa_bf[:, C:, :])
+        quantize(xa_codes[:, :C], xa_scales[:, :C], xa_bf[:, :C, :])
+        interleave(nc.scalar.copy, xb_bf[:], x_raw[:, :, A:])
 
         for g in range(G):
             rows = slice(R * g, R * (g + 1))
-            for c in range(A // C):
+            for c in (1, 2, 0):
                 cols = slice(C * c, C * (c + 1))
                 product(z[g][:, cols], w_mx[rows, :M], w_mx[rows, M:].bitcast(U8),
                         xa_codes[rows, cols], xa_scales[rows, cols], True, True)
@@ -159,7 +166,7 @@ def tile_rows_pl_mix_hyena_kernel(tc, x, w, dd, xs, x1, out_0, out_1, out_2):
             binary(ADD, summed[k][:, g, :], z[g][:, starts[k] : starts[k] + widths[k]], direct[k][:, g, :])
 
         def gate_round_move(k, g):
-            binary(MULT, y[k][:, g, :], summed[k][:, g, :], x1_a[:, g, starts[k] : starts[k] + widths[k]])
+            binary(MULT, y[k][:, g, :], summed[k][:, g, :], x1_a[g // 2][:, g % 2, starts[k] : starts[k] + widths[k]])
             nc.scalar.copy(out=y_bf[k][g][:], in_=y[k][:, g, :])
             nc.sync.dma_start(out=y_moved[k][R * g : R * (g + 1)], in_=y_bf[k][g][:])
 
@@ -170,17 +177,6 @@ def tile_rows_pl_mix_hyena_kernel(tc, x, w, dd, xs, x1, out_0, out_1, out_2):
         nc.sync.dma_start(out=xs_b[:], in_=xs_packed[:, :, A:])
         nc.sync.dma_start(out=x1_b[:], in_=x1_packed[:, :, A:])
         direct_term(0, 1)
-        add_direct(0, 0)
-        quantize(wd_codes[:], wd_scales[:].bitcast(U8), wd_bf[:])
-        add_direct(0, 1)
-        nc.vector.tensor_copy(
-            out=wz_codes[:, PAD:].rearrange("p (u m) -> p u m", u=PACK)[:, :, :R],
-            in_=wd_codes[:].rearrange("p (u i) -> p u i", u=PACK),
-        )
-        nc.vector.tensor_copy(
-            out=wz_scales[:, 16:80].rearrange("p (u r i) -> p u r i", u=PACK, r=2),
-            in_=wd_scales[:].rearrange("p (u i) -> p u i", u=PACK).unsqueeze(2).to_broadcast([R, PACK, 2, 8]),
-        )
         for u in range(PACK):
             for g in range(G):
                 first = PAD + M * u - R * g
@@ -189,7 +185,7 @@ def tile_rows_pl_mix_hyena_kernel(tc, x, w, dd, xs, x1, out_0, out_1, out_2):
                         wz_scales[:, first_scale : first_scale + M // 4].bitcast(U8),
                         xb_copy[g][:R, :C], xb_copy[g][:R, C:].bitcast(U8), g == 0, g == G - 1)
 
-        for g in range(2, G):
+        for g in range(G):
             add_direct(0, g)
         for g in range(G):
             gate_round_move(0, g)

@@ -22,6 +22,7 @@ A1 = 2 * C
 X_SCALAR = 128
 Y_VECTOR = 80
 PAD = M - R
+ORDER = (0, 2, 1, 3)
 
 
 def interleave(engine_copy, dst, src):
@@ -110,7 +111,7 @@ def tile_rows_pl_mix_hyena_kernel(tc, x, w, dd, xs, x1, out_0, out_1, out_2):
         )
         nc.sync.dma_start(out=x_raw[:], in_=x_rows)
         for a in range(2):
-            nc.sync.dma_start(out=xs_a[a][:], in_=xs_plain[:, 2 * a : 2 * a + 2, :A])
+            nc.sync.dma_start(out=xs_a[a][:], in_=xs_plain[:, a::2, :A])
 
         nc.vector.memset(w_mx[:R, M:], 0)
         nc.vector.memset(xb_mx[:, C:], 0)
@@ -129,11 +130,11 @@ def tile_rows_pl_mix_hyena_kernel(tc, x, w, dd, xs, x1, out_0, out_1, out_2):
         )
         nc.vector.transpose(out=dd_all[:], in_=dd_wide[:])
         quantize(w_mx[:R, :M], w_mx[:R, M:].bitcast(U8), w_bf[:])
-        for g in range(1, G):
-            queue = nc.scalar if g == 1 else nc.sync
+        for g in ORDER[1:]:
+            queue = nc.scalar if g == ORDER[1] else nc.sync
             queue.dma_start(out=w_mx[R * g : R * (g + 1)], in_=w_mx[:R])
         for a in range(2):
-            nc.sync.dma_start(out=x1_a[a][:], in_=x1_plain[:, 2 * a : 2 * a + 2, :A])
+            nc.sync.dma_start(out=x1_a[a][:], in_=x1_plain[:, a::2, :A])
         quantize(wd_codes[:], wd_scales[:].bitcast(U8), wd_bf[:])
 
         interleave(nc.scalar.copy, xa_bf[:, :X_SCALAR, :], x_raw[:, :, :X_SCALAR])
@@ -150,7 +151,7 @@ def tile_rows_pl_mix_hyena_kernel(tc, x, w, dd, xs, x1, out_0, out_1, out_2):
         quantize(xa_codes[:, :C], xa_scales[:, :C], xa_bf[:, :C, :])
         interleave(nc.scalar.copy, xb_bf[:], x_raw[:, :, A:])
 
-        for g in range(G):
+        for g in ORDER:
             rows = slice(R * g, R * (g + 1))
             for c in (1, 2, 0):
                 cols = slice(C * c, C * (c + 1))
@@ -159,16 +160,17 @@ def tile_rows_pl_mix_hyena_kernel(tc, x, w, dd, xs, x1, out_0, out_1, out_2):
 
         def direct_term(k, a):
             cols = slice(starts[k], starts[k] + widths[k])
-            binary(MULT, direct[k][:, 2 * a : 2 * a + 2, :], xs_a[a][:, :, cols],
+            binary(MULT, direct[k][:, a::2, :], xs_a[a][:, :, cols],
                    dd_all[:, cols].unsqueeze(1).to_broadcast([P, 2, widths[k]]))
 
         def add_direct(k, g):
             binary(ADD, summed[k][:, g, :], z[g][:, starts[k] : starts[k] + widths[k]], direct[k][:, g, :])
 
         def gate_round_move(k, g):
-            binary(MULT, y[k][:, g, :], summed[k][:, g, :], x1_a[g // 2][:, g % 2, starts[k] : starts[k] + widths[k]])
+            binary(MULT, y[k][:, g, :], summed[k][:, g, :], x1_a[g % 2][:, g // 2, starts[k] : starts[k] + widths[k]])
             nc.scalar.copy(out=y_bf[k][g][:], in_=y[k][:, g, :])
-            nc.sync.dma_start(out=y_moved[k][R * g : R * (g + 1)], in_=y_bf[k][g][:])
+            queue = nc.scalar if (k, g) == (0, ORDER[-1]) else nc.sync
+            queue.dma_start(out=y_moved[k][R * g : R * (g + 1)], in_=y_bf[k][g][:])
 
         direct_term(0, 0)
         quantize(xb_mx[:, :C], xb_mx[:, C:].bitcast(U8), xb_bf[:])
@@ -185,16 +187,16 @@ def tile_rows_pl_mix_hyena_kernel(tc, x, w, dd, xs, x1, out_0, out_1, out_2):
                         wz_scales[:, first_scale : first_scale + M // 4].bitcast(U8),
                         xb_copy[g][:R, :C], xb_copy[g][:R, C:].bitcast(U8), g == 0, g == G - 1)
 
-        for g in range(G):
+        for g in ORDER:
             add_direct(0, g)
-        for g in range(G):
+        for g in ORDER:
             gate_round_move(0, g)
-        nc.sync.dma_start(out=y_plain[:, :, :A1], in_=y[0][:])
+        nc.scalar.dma_start(out=y_plain[:, :, :A1], in_=y[0][:])
         for a in range(2):
             direct_term(1, a)
-        for g in range(G):
+        for g in ORDER:
             add_direct(1, g)
-        for g in range(G):
+        for g in ORDER:
             gate_round_move(1, g)
         nc.sync.dma_start(out=y_plain[:, :, A1:A], in_=y[1][:])
         interleave(nc.scalar.copy, y_words[0][:], y_moved[0][:])

@@ -19,7 +19,6 @@ PACK = 4
 C = 128
 A = 3 * C
 A1 = 2 * C
-X_SCALAR = 128
 Y_VECTOR = 80
 PAD = M - R
 ORDER = (0, 2, 1, 3)
@@ -90,6 +89,7 @@ def tile_rows_pl_mix_hyena_kernel(tc, x, w, dd, xs, x1, out_0, out_1, out_2):
         y_codes = [tile("y_codes%d" % h, [P, A1], I32) for h in range(2)]
         y_scales = tile("y_scales", [P, N], U8)
         z = [ps.tile([P, N], F32, name="z%d" % g) for g in range(G)]
+        z_late = [ps.tile([P, N], F32, name="z_late%d" % g)[:, :C] for g in range(G - 1)] + [z[G - 1][:, A1:A]]
         z_b = ps.tile([P, N], F32, name="z_b")
 
         def quantize(codes, scales, src):
@@ -137,8 +137,9 @@ def tile_rows_pl_mix_hyena_kernel(tc, x, w, dd, xs, x1, out_0, out_1, out_2):
             nc.sync.dma_start(out=x1_a[a][:], in_=x1_plain[:, a::2, :A])
         quantize(wd_codes[:], wd_scales[:].bitcast(U8), wd_bf[:])
 
-        interleave(nc.scalar.copy, xa_bf[:, :X_SCALAR, :], x_raw[:, :, :X_SCALAR])
-        interleave(nc.vector.tensor_copy, xa_bf[:, X_SCALAR:, :], x_raw[:, :, X_SCALAR:A])
+        interleave(nc.scalar.copy, xb_bf[:], x_raw[:, :, A:])
+        interleave(nc.scalar.copy, xa_bf[:, A1:, :], x_raw[:, :, A1:A])
+        interleave(nc.vector.tensor_copy, xa_bf[:, :A1, :], x_raw[:, :, :A1])
         nc.vector.tensor_copy(
             out=wz_codes[:, PAD:].rearrange("p (u m) -> p u m", u=PACK)[:, :, :R],
             in_=wd_codes[:].rearrange("p (u i) -> p u i", u=PACK),
@@ -147,16 +148,30 @@ def tile_rows_pl_mix_hyena_kernel(tc, x, w, dd, xs, x1, out_0, out_1, out_2):
             out=wz_scales[:, 16:80].rearrange("p (u r i) -> p u r i", u=PACK, r=2),
             in_=wd_scales[:].rearrange("p (u i) -> p u i", u=PACK).unsqueeze(2).to_broadcast([R, PACK, 2, 8]),
         )
-        quantize(xa_codes[:, C:], xa_scales[:, C:], xa_bf[:, C:, :])
-        quantize(xa_codes[:, :C], xa_scales[:, :C], xa_bf[:, :C, :])
-        interleave(nc.scalar.copy, xb_bf[:], x_raw[:, :, A:])
+        quantize(xa_codes[:, :A1], xa_scales[:, :A1], xa_bf[:, :A1, :])
+        quantize(xb_mx[:, :C], xb_mx[:, C:].bitcast(U8), xb_bf[:])
+        for g in range(1, G):
+            nc.scalar.dma_start(out=xb_copy[g][:], in_=xb_mx[R * g : R * (g + 1)])
 
-        for g in ORDER:
+        def plain_pass(g, c):
             rows = slice(R * g, R * (g + 1))
-            for c in (1, 2, 0):
-                cols = slice(C * c, C * (c + 1))
-                product(z[g][:, cols], w_mx[rows, :M], w_mx[rows, M:].bitcast(U8),
-                        xa_codes[rows, cols], xa_scales[rows, cols], True, True)
+            cols = slice(C * c, C * (c + 1))
+            out = z[g][:, cols] if c < 2 else z_late[g]
+            product(out, w_mx[rows, :M], w_mx[rows, M:].bitcast(U8),
+                    xa_codes[rows, cols], xa_scales[rows, cols], True, True)
+
+        def padded_passes(g):
+            for u in range(PACK):
+                first = PAD + M * u - R * g
+                first_scale = 16 + 16 * u - 16 * (g // 2)
+                product(z_b[:, C * u : C * (u + 1)], wz_codes[:, first : first + M],
+                        wz_scales[:, first_scale : first_scale + M // 4].bitcast(U8),
+                        xb_copy[g][:R, :C], xb_copy[g][:R, C:].bitcast(U8),
+                        (g, u) == (0, 0), (g, u) == (G - 1, PACK - 1))
+
+        for c in range(2):
+            plain_pass(0, c)
+            plain_pass(2, c)
 
         def direct_term(k, a):
             cols = slice(starts[k], starts[k] + widths[k])
@@ -164,7 +179,7 @@ def tile_rows_pl_mix_hyena_kernel(tc, x, w, dd, xs, x1, out_0, out_1, out_2):
                    dd_all[:, cols].unsqueeze(1).to_broadcast([P, 2, widths[k]]))
 
         def add_direct(k, g):
-            binary(ADD, summed[k][:, g, :], z[g][:, starts[k] : starts[k] + widths[k]], direct[k][:, g, :])
+            binary(ADD, summed[k][:, g, :], z[g][:, :A1] if k == 0 else z_late[g], direct[k][:, g, :])
 
         def gate_round_move(k, g):
             binary(MULT, y[k][:, g, :], summed[k][:, g, :], x1_a[g % 2][:, g // 2, starts[k] : starts[k] + widths[k]])
@@ -173,19 +188,17 @@ def tile_rows_pl_mix_hyena_kernel(tc, x, w, dd, xs, x1, out_0, out_1, out_2):
             queue.dma_start(out=y_moved[k][R * g : R * (g + 1)], in_=y_bf[k][g][:])
 
         direct_term(0, 0)
-        quantize(xb_mx[:, :C], xb_mx[:, C:].bitcast(U8), xb_bf[:])
-        for g in range(1, G):
-            nc.sync.dma_start(out=xb_copy[g][:], in_=xb_mx[R * g : R * (g + 1)])
+        quantize(xa_codes[:, A1:], xa_scales[:, A1:], xa_bf[:, A1:, :])
+        for c in range(2):
+            plain_pass(1, c)
+            plain_pass(3, c)
+        for g in ORDER[::-1]:
+            plain_pass(g, 2)
+        for g in range(G):
+            padded_passes(g)
         nc.sync.dma_start(out=xs_b[:], in_=xs_packed[:, :, A:])
         nc.sync.dma_start(out=x1_b[:], in_=x1_packed[:, :, A:])
         direct_term(0, 1)
-        for u in range(PACK):
-            for g in range(G):
-                first = PAD + M * u - R * g
-                first_scale = 16 + 16 * u - 16 * (g // 2)
-                product(z_b[:, C * u : C * (u + 1)], wz_codes[:, first : first + M],
-                        wz_scales[:, first_scale : first_scale + M // 4].bitcast(U8),
-                        xb_copy[g][:R, :C], xb_copy[g][:R, C:].bitcast(U8), g == 0, g == G - 1)
 
         for g in ORDER:
             add_direct(0, g)

@@ -151,7 +151,8 @@ def tile_rows_pl_mix_hyena_kernel(tc, x, w, dd, xs, x1, out_0, out_1, out_2):
         quantize(xa_codes[:, :A1], xa_scales[:, :A1], xa_bf[:, :A1, :])
         quantize(xb_mx[:, :C], xb_mx[:, C:].bitcast(U8), xb_bf[:])
         for g in range(1, G):
-            nc.scalar.dma_start(out=xb_copy[g][:], in_=xb_mx[R * g : R * (g + 1)])
+            queue = nc.sync if g == G - 1 else nc.scalar
+            queue.dma_start(out=xb_copy[g][:], in_=xb_mx[R * g : R * (g + 1)])
 
         def plain_pass(g, c):
             rows = slice(R * g, R * (g + 1))

@@ -17,9 +17,10 @@ P = 128
 R = 32
 PACK = 4
 C = 128
-A = 3 * C
-A1 = 2 * C
-Y_VECTOR = 80
+A = 2 * C
+B = N - A
+Y_VECTOR = 144
+MX = C + C // 4
 PAD = M - R
 ORDER = (0, 2, 1, 3)
 
@@ -54,43 +55,40 @@ def tile_rows_pl_mix_hyena_kernel(tc, x, w, dd, xs, x1, out_0, out_1, out_2):
 
         w_raw = tile("w_raw", [R, PACK, M], F32)
         w_bf = tile("w_bf", [R, M, PACK], BF16)
-        w_mx = tile("w_mx", [P, M + M // 4], I32)
         wd_bf = tile("wd_bf", [R, M, PACK], BF16)
-        wd_codes = tile("wd_codes", [R, M], I32)
-        wd_scales = tile("wd_scales", [R, M // 4], I32)
-        wz_codes = tile("wz_codes", [R, PAD + PACK * M], I32)
-        wz_scales = tile("wz_scales", [R, 96], I32)
+        w_mx = tile("w_mx", [P, 2, MX], I32)
+        wz_codes = tile("wz_codes", [2 * R, PAD + PACK * M], I32)
+        wz_scales = tile("wz_scales", [2 * R, 96], I32)
         dd_rows = tile("dd_rows", [P, R], F32)
         dd_cols = tile("dd_cols", [P, R], F32)
         dd_wide = tile("dd_wide", [P, N], F32)
         dd_all = tile("dd_all", [P, N], F32)
         x_raw = tile("x_raw", [P, PACK, N], F32)
         xa_bf = tile("xa_bf", [P, A, PACK], BF16)
-        xb_bf = tile("xb_bf", [P, C, PACK], BF16)
+        xb_bf = [tile("xb_bf%d" % t, [P, C, PACK], BF16) for t in range(2)]
         xa_codes = tile("xa_codes", [P, A], I32)
         xa_scales = tile("xa_scales", [P, A], U8)
-        xb_mx = tile("xb_mx", [P, C + C // 4], I32)
-        xb_copy = [xb_mx] + [tile("xb_copy%d" % g, [R, C + C // 4], I32) for g in range(1, G)]
-        xs_a = [tile("xs_a%d" % a, [P, 2, A], F32) for a in range(2)]
-        x1_a = [tile("x1_a%d" % a, [P, 2, A], F32) for a in range(2)]
-        xs_b = tile("xs_b", [P, PACK, C], F32)
-        x1_b = tile("x1_b", [P, PACK, C], F32)
-        widths = (A1, C)
-        starts = (0, A1)
-        direct = [tile("direct%d" % k, [P, G, widths[k]], F32) for k in range(2)]
-        summed = [tile("summed%d" % k, [P, G, widths[k]], F32) for k in range(2)]
-        y = [tile("y%d" % k, [P, G, widths[k]], F32) for k in range(2)]
-        y_bf = [[tile("y_bf%d_%d" % (k, g), [P, widths[k]], BF16) for g in range(G)] for k in range(2)]
-        y_moved = [tile("y_moved%d" % k, [P, PACK, widths[k]], BF16) for k in range(2)]
-        direct_b = tile("direct_b", [P, PACK, C], F32)
-        summed_b = tile("summed_b", [P, PACK, C], F32)
-        y_b = tile("y_b", [P, PACK, C], F32)
-        y_words = [tile("y_words%d" % h, [P, A1, PACK], BF16) for h in range(2)]
-        y_codes = [tile("y_codes%d" % h, [P, A1], I32) for h in range(2)]
+        xb_mx = [tile("xb_mx%d" % t, [P, MX], I32) for t in range(2)]
+        xb_copy = [
+            [xb_mx[t] if g == t else tile("xb_copy%d_%d" % (t, g), [2 * R, MX], I32) for g in range(G)] for t in range(2)
+        ]
+        xs_a = tile("xs_a", [P, G, A], F32)
+        x1_a = tile("x1_a", [P, G, A], F32)
+        xs_b = [tile("xs_b%d" % h, [P, 2, B], F32) for h in range(2)]
+        x1_b = [tile("x1_b%d" % h, [P, 2, B], F32) for h in range(2)]
+        direct = tile("direct", [P, G, A], F32)
+        summed = tile("summed", [P, G, A], F32)
+        y_a = tile("y_a", [P, G, A], F32)
+        y_bf = [tile("y_bf%d" % g, [P, A], BF16) for g in range(G)]
+        y_moved = tile("y_moved", [P, PACK, A], BF16)
+        direct_b = tile("direct_b", [P, PACK, B], F32)
+        summed_b = tile("summed_b", [P, PACK, B], F32)
+        y_b = tile("y_b", [P, PACK, B], F32)
+        y_words = [tile("y_words%d" % h, [P, A, PACK], BF16) for h in range(2)]
+        y_codes = [tile("y_codes%d" % h, [P, A], I32) for h in range(2)]
         y_scales = tile("y_scales", [P, N], U8)
         z = [ps.tile([P, N], F32, name="z%d" % g) for g in range(G)]
-        z_late = [ps.tile([P, N], F32, name="z_late%d" % g)[:, :C] for g in range(G - 1)] + [z[G - 1][:, A1:A]]
-        z_b = ps.tile([P, N], F32, name="z_b")
+        z_b = [[ps.tile([P, N], F32, name="z_b%d_%d" % (h, t)) for t in range(2)] for h in range(2)]
 
         def quantize(codes, scales, src):
             nc.vector.quantize_mx(out=codes.bitcast(FP8X4), scales=scales, in_=src.rearrange("p c j -> p (c j)"))
@@ -110,14 +108,13 @@ def tile_rows_pl_mix_hyena_kernel(tc, x, w, dd, xs, x1, out_0, out_1, out_2):
             in_=dd.rearrange("o (b i) -> o b i", i=R).broadcast_to([P // 16, 16, R]),
         )
         nc.sync.dma_start(out=x_raw[:], in_=x_rows)
-        for a in range(2):
-            nc.sync.dma_start(out=xs_a[a][:], in_=xs_plain[:, a::2, :A])
+        nc.sync.dma_start(out=xs_a[:], in_=xs_plain[:, :, :A])
 
-        nc.vector.memset(w_mx[:R, M:], 0)
-        nc.vector.memset(xb_mx[:, C:], 0)
+        nc.vector.memset(w_mx[:R, :, M:], 0)
+        for t in range(2):
+            nc.vector.memset(xb_mx[t][:, C:], 0)
         nc.vector.memset(wz_codes[:], 0)
         nc.vector.memset(wz_scales[:], 0)
-        nc.vector.memset(wd_scales[:], 0)
         nc.vector.transpose(out=dd_cols[:], in_=dd_rows[:])
         interleave(nc.scalar.copy, w_bf[:], w_raw[:])
         nc.vector.tensor_copy(
@@ -129,109 +126,100 @@ def tile_rows_pl_mix_hyena_kernel(tc, x, w, dd, xs, x1, out_0, out_1, out_2):
             in_=w_raw[:].rearrange("p j (i u) -> p u i j", u=PACK),
         )
         nc.vector.transpose(out=dd_all[:], in_=dd_wide[:])
-        quantize(w_mx[:R, :M], w_mx[:R, M:].bitcast(U8), w_bf[:])
-        for g in ORDER[1:]:
-            queue = nc.scalar if g == ORDER[1] else nc.sync
-            queue.dma_start(out=w_mx[R * g : R * (g + 1)], in_=w_mx[:R])
-        for a in range(2):
-            nc.sync.dma_start(out=x1_a[a][:], in_=x1_plain[:, a::2, :A])
-        quantize(wd_codes[:], wd_scales[:].bitcast(U8), wd_bf[:])
+        quantize(w_mx[:R, 0, :M], w_mx[:R, 0, M:].bitcast(U8), w_bf[:])
+        for g in (2, 3):
+            queue = nc.scalar if g == 2 else nc.sync
+            queue.dma_start(out=w_mx[R * g : R * (g + 1), 0, :], in_=w_mx[:R, 0, :])
+        quantize(w_mx[:R, 1, :M], w_mx[:R, 1, M:].bitcast(U8), wd_bf[:])
+        nc.sync.dma_start(out=w_mx[R : 2 * R], in_=w_mx[:R])
+        nc.sync.dma_start(out=x1_a[:], in_=x1_plain[:, :, :A])
 
-        interleave(nc.scalar.copy, xb_bf[:], x_raw[:, :, A:])
-        interleave(nc.scalar.copy, xa_bf[:, A1:, :], x_raw[:, :, A1:A])
-        interleave(nc.vector.tensor_copy, xa_bf[:, :A1, :], x_raw[:, :, :A1])
-        nc.vector.tensor_copy(
-            out=wz_codes[:, PAD:].rearrange("p (u m) -> p u m", u=PACK)[:, :, :R],
-            in_=wd_codes[:].rearrange("p (u i) -> p u i", u=PACK),
-        )
-        nc.vector.tensor_copy(
-            out=wz_scales[:, 16:80].rearrange("p (u r i) -> p u r i", u=PACK, r=2),
-            in_=wd_scales[:].rearrange("p (u i) -> p u i", u=PACK).unsqueeze(2).to_broadcast([R, PACK, 2, 8]),
-        )
-        quantize(xa_codes[:, :A1], xa_scales[:, :A1], xa_bf[:, :A1, :])
-        quantize(xb_mx[:, :C], xb_mx[:, C:].bitcast(U8), xb_bf[:])
-        for g in range(1, G):
-            queue = nc.sync if g == G - 1 else nc.scalar
-            queue.dma_start(out=xb_copy[g][:], in_=xb_mx[R * g : R * (g + 1)])
+        for t in range(2):
+            interleave(nc.scalar.copy, xb_bf[t][:], x_raw[:, :, A + C * t : A + C * (t + 1)])
+        interleave(nc.vector.tensor_copy, xa_bf[:], x_raw[:, :, :A])
+
+        def quantize_and_copy(t):
+            quantize(xb_mx[t][:, :C], xb_mx[t][:, C:].bitcast(U8), xb_bf[t][:])
+            for g in range(G):
+                if g != t:
+                    nc.sync.dma_start(out=xb_copy[t][g][R * t : R * (t + 1)], in_=xb_mx[t][R * g : R * (g + 1)])
 
         def plain_pass(g, c):
             rows = slice(R * g, R * (g + 1))
             cols = slice(C * c, C * (c + 1))
-            out = z[g][:, cols] if c < 2 else z_late[g]
-            product(out, w_mx[rows, :M], w_mx[rows, M:].bitcast(U8),
+            product(z[g][:, cols], w_mx[rows, 0, :M], w_mx[rows, 0, M:].bitcast(U8),
                     xa_codes[rows, cols], xa_scales[rows, cols], True, True)
 
-        def padded_passes(g):
-            for u in range(PACK):
-                first = PAD + M * u - R * g
-                first_scale = 16 + 16 * u - 16 * (g // 2)
-                product(z_b[:, C * u : C * (u + 1)], wz_codes[:, first : first + M],
-                        wz_scales[:, first_scale : first_scale + M // 4].bitcast(U8),
-                        xb_copy[g][:R, :C], xb_copy[g][:R, C:].bitcast(U8),
-                        (g, u) == (0, 0), (g, u) == (G - 1, PACK - 1))
+        def padded_pass(t, g, u, start, stop):
+            rows = slice(R * t, R * (t + 1))
+            first = PAD + M * u - R * g
+            first_scale = 16 + 16 * u - 16 * (g // 2)
+            product(z_b[u // 2][t][:, C * (u % 2) : C * (u % 2 + 1)], wz_codes[rows, first : first + M],
+                    wz_scales[rows, first_scale : first_scale + M // 4].bitcast(U8),
+                    xb_copy[t][g][rows, :C], xb_copy[t][g][rows, C:].bitcast(U8), start, stop)
 
-        for c in range(2):
-            plain_pass(0, c)
-            plain_pass(2, c)
+        def direct_term(a):
+            binary(MULT, direct[:, a::2, :], xs_a[:, a::2, :], dd_all[:, :A].unsqueeze(1).to_broadcast([P, 2, A]))
 
-        def direct_term(k, a):
-            cols = slice(starts[k], starts[k] + widths[k])
-            binary(MULT, direct[k][:, a::2, :], xs_a[a][:, :, cols],
-                   dd_all[:, cols].unsqueeze(1).to_broadcast([P, 2, widths[k]]))
-
-        def add_direct(k, g):
-            binary(ADD, summed[k][:, g, :], z[g][:, :A1] if k == 0 else z_late[g], direct[k][:, g, :])
-
-        def gate_round_move(k, g):
-            binary(MULT, y[k][:, g, :], summed[k][:, g, :], x1_a[g % 2][:, g // 2, starts[k] : starts[k] + widths[k]])
-            nc.scalar.copy(out=y_bf[k][g][:], in_=y[k][:, g, :])
-            queue = nc.scalar if (k, g) == (0, ORDER[-1]) else nc.sync
-            queue.dma_start(out=y_moved[k][R * g : R * (g + 1)], in_=y_bf[k][g][:])
-
-        direct_term(0, 0)
-        quantize(xa_codes[:, A1:], xa_scales[:, A1:], xa_bf[:, A1:, :])
-        for c in range(2):
-            plain_pass(1, c)
-            plain_pass(3, c)
-        for g in ORDER[::-1]:
-            plain_pass(g, 2)
-        for g in range(G):
-            padded_passes(g)
-        nc.sync.dma_start(out=xs_b[:], in_=xs_packed[:, :, A:])
-        nc.sync.dma_start(out=x1_b[:], in_=x1_packed[:, :, A:])
-        direct_term(0, 1)
+        quantize_and_copy(0)
+        quantize(xa_codes[:], xa_scales[:], xa_bf[:])
+        for pair in (ORDER[:2], ORDER[2:]):
+            for c in range(A // C):
+                for g in pair:
+                    plain_pass(g, c)
+        quantize_and_copy(1)
+        nc.sync.dma_start(out=xs_b[0][:], in_=xs_packed[:, 0:2, A:])
+        nc.sync.dma_start(out=x1_b[0][:], in_=x1_packed[:, 0:2, A:])
+        nc.sync.dma_start(out=xs_b[1][:], in_=xs_packed[:, 2:4, A:])
+        direct_term(0)
+        nc.vector.tensor_copy(
+            out=wz_codes[:, PAD:].rearrange("p (u m) -> p u m", u=PACK)[:, :, :R],
+            in_=w_mx[: 2 * R, 1, :M].rearrange("p (u i) -> p u i", u=PACK),
+        )
+        nc.vector.tensor_copy(
+            out=wz_scales[:, 16:80].rearrange("p (u r i) -> p u r i", u=PACK, r=2),
+            in_=w_mx[: 2 * R, 1, M:].rearrange("p (u i) -> p u i", u=PACK).unsqueeze(2).to_broadcast([2 * R, PACK, 2, 8]),
+        )
+        binary(MULT, direct[:, 1, :], xs_a[:, 1, :], dd_all[:, :A])
+        nc.gpsimd.tensor_tensor(out=xs_a[:, 1, :], in0=xs_a[:, 3, :], in1=dd_all[:, :A], op=MULT)
+        for u in range(PACK):
+            for t in range(2):
+                padded_pass(t, t, u, u % 2 == 0, False)
+        for h in range(2):
+            for step in range(1, G):
+                for e in range(2):
+                    for t in range(2):
+                        padded_pass(t, (t + step) % G, 2 * h + e, False, (step, e) == (G - 1, 1))
 
         for g in ORDER:
-            add_direct(0, g)
+            binary(ADD, summed[:, g, :], z[g][:, :A], xs_a[:, 1, :] if g == 3 else direct[:, g, :])
         for g in ORDER:
-            gate_round_move(0, g)
-        nc.scalar.dma_start(out=y_plain[:, :, :A1], in_=y[0][:])
-        for a in range(2):
-            direct_term(1, a)
-        for g in ORDER:
-            add_direct(1, g)
-        for g in ORDER:
-            gate_round_move(1, g)
-        nc.sync.dma_start(out=y_plain[:, :, A1:A], in_=y[1][:])
-        interleave(nc.scalar.copy, y_words[0][:], y_moved[0][:])
+            binary(MULT, y_a[:, g, :], summed[:, g, :], x1_a[:, g, :])
+            nc.scalar.copy(out=y_bf[g][:], in_=y_a[:, g, :])
+            nc.sync.dma_start(out=y_moved[R * g : R * (g + 1)], in_=y_bf[g][:])
+        nc.sync.dma_start(out=x1_b[1][:], in_=x1_packed[:, 2:4, A:])
+        nc.sync.dma_start(out=y_plain[:, :, :A], in_=y_a[:])
+        interleave(nc.scalar.copy, y_words[0][:], y_moved[:])
 
-        halves = (slice(0, 2), slice(2, 4))
-        z_b_places = z_b[:].rearrange("p (u n) -> p u n", u=PACK)
-        for us in halves:
-            binary(MULT, direct_b[:, us, :], xs_b[:, us, :], dd_all[:, A:].unsqueeze(1).to_broadcast([P, 2, C]))
-        for us in halves:
-            binary(ADD, summed_b[:, us, :], z_b_places[:, us, :], direct_b[:, us, :])
-        for us in halves:
-            binary(MULT, y_b[:, us, :], summed_b[:, us, :], x1_b[:, us, :])
-        nc.sync.dma_start(out=y_packed[:, :, A:], in_=y_b[:])
-        quantize(y_codes[0][:], y_scales[:, :A1], y_words[0][:])
-        nc.sync.dma_start(out=words_out[:, :A1], in_=y_codes[0][:])
-        interleave(nc.vector.tensor_copy, y_words[1][:, C:, :], y_b[:])
-        interleave(nc.scalar.copy, y_words[1][:, Y_VECTOR:C, :], y_moved[1][:, :, Y_VECTOR:])
-        interleave(nc.vector.tensor_copy, y_words[1][:, :Y_VECTOR, :], y_moved[1][:, :, :Y_VECTOR])
-        quantize(y_codes[1][:, C:], y_scales[:, A:], y_words[1][:, C:, :])
-        quantize(y_codes[1][:, :C], y_scales[:, A1:A], y_words[1][:, :C, :])
-        nc.sync.dma_start(out=words_out[:, A1:], in_=y_codes[1][:])
+        for h in range(2):
+            us = slice(2 * h, 2 * h + 2)
+            for t in range(2):
+                cols = slice(C * t, C * (t + 1))
+                dd_cols_b = dd_all[:, A + C * t : A + C * (t + 1)].unsqueeze(1).to_broadcast([P, 2, C])
+                binary(MULT, direct_b[:, us, cols], xs_b[h][:, :, cols], dd_cols_b)
+            for t in range(2):
+                cols = slice(C * t, C * (t + 1))
+                binary(ADD, summed_b[:, us, cols], z_b[h][t][:, : 2 * C].rearrange("p (e n) -> p e n", e=2), direct_b[:, us, cols])
+            for t in range(2):
+                cols = slice(C * t, C * (t + 1))
+                binary(MULT, y_b[:, us, cols], summed_b[:, us, cols], x1_b[h][:, :, cols])
+            nc.sync.dma_start(out=y_packed[:, us, A:], in_=y_b[:, us, :])
+        interleave(nc.scalar.copy, y_words[1][:, Y_VECTOR:, :], y_b[:, :, Y_VECTOR:])
+        interleave(nc.vector.tensor_copy, y_words[1][:, :Y_VECTOR, :], y_b[:, :, :Y_VECTOR])
+        quantize(y_codes[0][:], y_scales[:, :A], y_words[0][:])
+        nc.sync.dma_start(out=words_out[:, :A], in_=y_codes[0][:])
+        quantize(y_codes[1][:], y_scales[:, A:], y_words[1][:])
+        nc.sync.dma_start(out=words_out[:, A:], in_=y_codes[1][:])
         for q in range(G):
             queue = nc.scalar if q % 2 == 0 else nc.sync
             queue.dma_start(out=scales_out[4 * q : 4 * q + 4, :], in_=y_scales[R * q : R * q + 4, :].bitcast(I32))

@@ -19,7 +19,7 @@ PACK = 4
 C = 128
 A = 2 * C
 B = N - A
-Y_VECTOR = 144
+Y_SCALAR = 88
 MX = C + C // 4
 PAD = M - R
 ORDER = (0, 2, 1, 3)
@@ -142,7 +142,8 @@ def tile_rows_pl_mix_hyena_kernel(tc, x, w, dd, xs, x1, out_0, out_1, out_2):
             quantize(xb_mx[t][:, :C], xb_mx[t][:, C:].bitcast(U8), xb_bf[t][:])
             for g in range(G):
                 if g != t:
-                    nc.sync.dma_start(out=xb_copy[t][g][R * t : R * (t + 1)], in_=xb_mx[t][R * g : R * (g + 1)])
+                    queue = nc.gpsimd if (t, g) == (0, G - 1) else nc.sync
+                    queue.dma_start(out=xb_copy[t][g][R * t : R * (t + 1)], in_=xb_mx[t][R * g : R * (g + 1)])
 
         def plain_pass(g, c):
             rows = slice(R * g, R * (g + 1))
@@ -214,8 +215,8 @@ def tile_rows_pl_mix_hyena_kernel(tc, x, w, dd, xs, x1, out_0, out_1, out_2):
                 cols = slice(C * t, C * (t + 1))
                 binary(MULT, y_b[:, us, cols], summed_b[:, us, cols], x1_b[h][:, :, cols])
             nc.sync.dma_start(out=y_packed[:, us, A:], in_=y_b[:, us, :])
-        interleave(nc.scalar.copy, y_words[1][:, Y_VECTOR:, :], y_b[:, :, Y_VECTOR:])
-        interleave(nc.vector.tensor_copy, y_words[1][:, :Y_VECTOR, :], y_b[:, :, :Y_VECTOR])
+        interleave(nc.scalar.copy, y_words[1][:, :Y_SCALAR, :], y_b[:, :, :Y_SCALAR])
+        interleave(nc.vector.tensor_copy, y_words[1][:, Y_SCALAR:, :], y_b[:, :, Y_SCALAR:])
         quantize(y_codes[0][:], y_scales[:, :A], y_words[0][:])
         nc.sync.dma_start(out=words_out[:, :A], in_=y_codes[0][:])
         quantize(y_codes[1][:], y_scales[:, A:], y_words[1][:])

@@ -51,7 +51,7 @@ def tile_rows_pl_mix_hyena_kernel(tc, x, w, dd, xs, x1, out_0, out_1, out_2):
         ctx.enter_context(tc.manual_schedule())
 
         def tile(name, shape, dtype):
-            return sb.tile(shape, dtype, name=name, align_bytes=64)
+            return sb.tile(shape, dtype, name=name, align_bytes=256)
 
         w_raw = tile("w_raw", [R, PACK, M], F32)
         w_bf = tile("w_bf", [R, M, PACK], BF16)
@@ -140,10 +140,10 @@ def tile_rows_pl_mix_hyena_kernel(tc, x, w, dd, xs, x1, out_0, out_1, out_2):
 
         def quantize_and_copy(t):
             quantize(xb_mx[t][:, :C], xb_mx[t][:, C:].bitcast(U8), xb_bf[t][:])
-            for g in range(G):
-                if g != t:
-                    queue = nc.gpsimd if (t, g) == (0, G - 1) else nc.sync
-                    queue.dma_start(out=xb_copy[t][g][R * t : R * (t + 1)], in_=xb_mx[t][R * g : R * (g + 1)])
+            for step in range(1, G):
+                g = (t + step) % G
+                queue = nc.gpsimd if (t, step) == (0, G - 1) else nc.sync
+                queue.dma_start(out=xb_copy[t][g][R * t : R * (t + 1)], in_=xb_mx[t][R * g : R * (g + 1)])
 
         def plain_pass(g, c):
             rows = slice(R * g, R * (g + 1))

@@ -8,6 +8,7 @@ FLOPS = 2 * G * D * M * N
 F32 = mybir.dt.float32
 BF16 = mybir.dt.bfloat16
 I32 = mybir.dt.int32
+U32 = mybir.dt.uint32
 U8 = mybir.dt.uint8
 FP8X4 = mybir.dt.float8_e4m3fn_x4
 ADD = mybir.AluOpType.add
@@ -19,7 +20,6 @@ PACK = 4
 C = 128
 A = 2 * C
 B = N - A
-Y_SCALAR = 88
 MX = C + C // 4
 PAD = M - R
 ORDER = (0, 2, 1, 3)
@@ -73,7 +73,7 @@ def tile_rows_pl_mix_hyena_kernel(tc, x, w, dd, xs, x1, out_0, out_1, out_2):
             [xb_mx[t] if g == t else tile("xb_copy%d_%d" % (t, g), [2 * R, MX], I32) for g in range(G)] for t in range(2)
         ]
         xs_a = tile("xs_a", [P, G, A], F32)
-        x1_a = tile("x1_a", [P, G, A], F32)
+        x1_a = [tile("x1_a%d" % a, [P, 2, A], F32) for a in range(2)]
         xs_b = [tile("xs_b%d" % h, [P, 2, B], F32) for h in range(2)]
         x1_b = [tile("x1_b%d" % h, [P, 2, B], F32) for h in range(2)]
         direct = tile("direct", [P, G, A], F32)
@@ -81,7 +81,7 @@ def tile_rows_pl_mix_hyena_kernel(tc, x, w, dd, xs, x1, out_0, out_1, out_2):
         y_a = tile("y_a", [P, G, A], F32)
         y_bf = [tile("y_bf%d" % g, [P, A], BF16) for g in range(G)]
         y_moved = tile("y_moved", [P, PACK, A], BF16)
-        direct_b = tile("direct_b", [P, PACK, B], F32)
+        direct_b = tile("direct_b", [P, 2, B], F32)
         summed_b = tile("summed_b", [P, PACK, B], F32)
         y_b = tile("y_b", [P, PACK, B], F32)
         y_words = [tile("y_words%d" % h, [P, A, PACK], BF16) for h in range(2)]
@@ -132,7 +132,8 @@ def tile_rows_pl_mix_hyena_kernel(tc, x, w, dd, xs, x1, out_0, out_1, out_2):
             queue.dma_start(out=w_mx[R * g : R * (g + 1), 0, :], in_=w_mx[:R, 0, :])
         quantize(w_mx[:R, 1, :M], w_mx[:R, 1, M:].bitcast(U8), wd_bf[:])
         nc.sync.dma_start(out=w_mx[R : 2 * R], in_=w_mx[:R])
-        nc.sync.dma_start(out=x1_a[:], in_=x1_plain[:, :, :A])
+        nc.sync.dma_start(out=xs_b[0][:], in_=xs_packed[:, 0:2, A:])
+        nc.sync.dma_start(out=x1_a[0][:], in_=x1_plain[:, 0::2, :A])
 
         for t in range(2):
             interleave(nc.scalar.copy, xb_bf[t][:], x_raw[:, :, A + C * t : A + C * (t + 1)])
@@ -159,9 +160,6 @@ def tile_rows_pl_mix_hyena_kernel(tc, x, w, dd, xs, x1, out_0, out_1, out_2):
                     wz_scales[rows, first_scale : first_scale + M // 4].bitcast(U8),
                     xb_copy[t][g][rows, :C], xb_copy[t][g][rows, C:].bitcast(U8), start, stop)
 
-        def direct_term(a):
-            binary(MULT, direct[:, a::2, :], xs_a[:, a::2, :], dd_all[:, :A].unsqueeze(1).to_broadcast([P, 2, A]))
-
         quantize_and_copy(0)
         quantize(xa_codes[:], xa_scales[:], xa_bf[:])
         for pair in (ORDER[:2], ORDER[2:]):
@@ -169,20 +167,22 @@ def tile_rows_pl_mix_hyena_kernel(tc, x, w, dd, xs, x1, out_0, out_1, out_2):
                 for g in pair:
                     plain_pass(g, c)
         quantize_and_copy(1)
-        nc.sync.dma_start(out=xs_b[0][:], in_=xs_packed[:, 0:2, A:])
-        nc.sync.dma_start(out=x1_b[0][:], in_=x1_packed[:, 0:2, A:])
+        nc.sync.dma_start(out=x1_a[1][:], in_=x1_plain[:, 1::2, :A])
         nc.sync.dma_start(out=xs_b[1][:], in_=xs_packed[:, 2:4, A:])
-        direct_term(0)
-        nc.vector.tensor_copy(
-            out=wz_codes[:, PAD:].rearrange("p (u m) -> p u m", u=PACK)[:, :, :R],
-            in_=w_mx[: 2 * R, 1, :M].rearrange("p (u i) -> p u i", u=PACK),
+        for h in range(2):
+            nc.sync.dma_start(out=x1_b[h][:], in_=x1_packed[:, 2 * h : 2 * h + 2, A:])
+        nc.scalar.copy(
+            out=wz_codes[:, PAD:].bitcast(U32).rearrange("p (u m) -> p u m", u=PACK)[:, :, :R],
+            in_=w_mx[: 2 * R, 1, :M].bitcast(U32).rearrange("p (u i) -> p u i", u=PACK),
         )
-        nc.vector.tensor_copy(
-            out=wz_scales[:, 16:80].rearrange("p (u r i) -> p u r i", u=PACK, r=2),
-            in_=w_mx[: 2 * R, 1, M:].rearrange("p (u i) -> p u i", u=PACK).unsqueeze(2).to_broadcast([2 * R, PACK, 2, 8]),
+        nc.scalar.copy(
+            out=wz_scales[:, 16:80].bitcast(U32).rearrange("p (u r i) -> p u r i", u=PACK, r=2),
+            in_=w_mx[: 2 * R, 1, M:].bitcast(U32).rearrange("p (u i) -> p u i", u=PACK).unsqueeze(2).to_broadcast([2 * R, PACK, 2, 8]),
         )
-        binary(MULT, direct[:, 1, :], xs_a[:, 1, :], dd_all[:, :A])
-        nc.gpsimd.tensor_tensor(out=xs_a[:, 1, :], in0=xs_a[:, 3, :], in1=dd_all[:, :A], op=MULT)
+        binary(MULT, direct[:], xs_a[:], dd_all[:, :A].unsqueeze(1).to_broadcast([P, G, A]))
+        dd_b = dd_all[:, A:].unsqueeze(1).to_broadcast([P, 2, B])
+        nc.gpsimd.tensor_tensor(out=xs_a[:, 0:2, :], in0=xs_b[0][:], in1=dd_b, op=MULT)
+        direct_pair = (xs_a[:, 0:2, :], direct_b[:])
         for u in range(PACK):
             for t in range(2):
                 padded_pass(t, t, u, u % 2 == 0, False)
@@ -193,30 +193,26 @@ def tile_rows_pl_mix_hyena_kernel(tc, x, w, dd, xs, x1, out_0, out_1, out_2):
                         padded_pass(t, (t + step) % G, 2 * h + e, False, (step, e) == (G - 1, 1))
 
         for g in ORDER:
-            binary(ADD, summed[:, g, :], z[g][:, :A], xs_a[:, 1, :] if g == 3 else direct[:, g, :])
+            binary(ADD, summed[:, g, :], z[g][:, :A], direct[:, g, :])
         for g in ORDER:
-            binary(MULT, y_a[:, g, :], summed[:, g, :], x1_a[:, g, :])
+            binary(MULT, y_a[:, g, :], summed[:, g, :], x1_a[g % 2][:, g // 2, :])
             nc.scalar.copy(out=y_bf[g][:], in_=y_a[:, g, :])
             nc.sync.dma_start(out=y_moved[R * g : R * (g + 1)], in_=y_bf[g][:])
-        nc.sync.dma_start(out=x1_b[1][:], in_=x1_packed[:, 2:4, A:])
         nc.sync.dma_start(out=y_plain[:, :, :A], in_=y_a[:])
         interleave(nc.scalar.copy, y_words[0][:], y_moved[:])
 
-        for h in range(2):
-            us = slice(2 * h, 2 * h + 2)
-            for t in range(2):
-                cols = slice(C * t, C * (t + 1))
-                dd_cols_b = dd_all[:, A + C * t : A + C * (t + 1)].unsqueeze(1).to_broadcast([P, 2, C])
-                binary(MULT, direct_b[:, us, cols], xs_b[h][:, :, cols], dd_cols_b)
-            for t in range(2):
-                cols = slice(C * t, C * (t + 1))
-                binary(ADD, summed_b[:, us, cols], z_b[h][t][:, : 2 * C].rearrange("p (e n) -> p e n", e=2), direct_b[:, us, cols])
-            for t in range(2):
-                cols = slice(C * t, C * (t + 1))
-                binary(MULT, y_b[:, us, cols], summed_b[:, us, cols], x1_b[h][:, :, cols])
-            nc.sync.dma_start(out=y_packed[:, us, A:], in_=y_b[:, us, :])
-        interleave(nc.scalar.copy, y_words[1][:, :Y_SCALAR, :], y_b[:, :, :Y_SCALAR])
-        interleave(nc.vector.tensor_copy, y_words[1][:, Y_SCALAR:, :], y_b[:, :, Y_SCALAR:])
+        binary(MULT, direct_b[:], xs_b[1][:], dd_b)
+        units = [(h, slice(2 * h, 2 * h + 2), t, slice(C * t, C * (t + 1))) for h in range(2) for t in range(2)]
+        for h, us, t, cols in units:
+            binary(ADD, summed_b[:, us, cols], z_b[h][t][:, : 2 * C].rearrange("p (e n) -> p e n", e=2), direct_pair[h][:, :, cols])
+        for h, us, t, cols in units:
+            engine = nc.gpsimd if (h, t) == (0, 0) else nc.vector
+            engine.tensor_tensor(out=y_b[:, us, cols], in0=summed_b[:, us, cols], in1=x1_b[h][:, :, cols], op=MULT)
+            if t == 1:
+                nc.sync.dma_start(out=y_packed[:, us, A:], in_=y_b[:, us, :])
+        for t in range(2):
+            cols = slice(C * t, C * (t + 1))
+            interleave(nc.vector.tensor_copy, y_words[1][:, cols, :], y_b[:, :, cols])
         quantize(y_codes[0][:], y_scales[:, :A], y_words[0][:])
         nc.sync.dma_start(out=words_out[:, :A], in_=y_codes[0][:])
         quantize(y_codes[1][:], y_scales[:, A:], y_words[1][:])

@@ -20,6 +20,8 @@ PACK = 4
 C = 128
 A = 2 * C
 B = N - A
+X_VECTOR = 64
+Y_VECTOR = 40
 MX = C + C // 4
 PAD = M - R
 ORDER = (0, 2, 1, 3)
@@ -76,12 +78,12 @@ def tile_rows_pl_mix_hyena_kernel(tc, x, w, dd, xs, x1, out_0, out_1, out_2):
         x1_a = [tile("x1_a%d" % a, [P, 2, A], F32) for a in range(2)]
         xs_b = [tile("xs_b%d" % h, [P, 2, B], F32) for h in range(2)]
         x1_b = [tile("x1_b%d" % h, [P, 2, B], F32) for h in range(2)]
-        direct = tile("direct", [P, G, A], F32)
+        direct = tile("direct", [P, G - 1, A], F32)
         summed = tile("summed", [P, G, A], F32)
         y_a = tile("y_a", [P, G, A], F32)
         y_bf = [tile("y_bf%d" % g, [P, A], BF16) for g in range(G)]
         y_moved = tile("y_moved", [P, PACK, A], BF16)
-        direct_b = tile("direct_b", [P, 2, B], F32)
+        direct_b = tile("direct_b", [P, PACK, B], F32)
         summed_b = tile("summed_b", [P, PACK, B], F32)
         y_b = tile("y_b", [P, PACK, B], F32)
         y_words = [tile("y_words%d" % h, [P, A, PACK], BF16) for h in range(2)]
@@ -132,12 +134,13 @@ def tile_rows_pl_mix_hyena_kernel(tc, x, w, dd, xs, x1, out_0, out_1, out_2):
             queue.dma_start(out=w_mx[R * g : R * (g + 1), 0, :], in_=w_mx[:R, 0, :])
         quantize(w_mx[:R, 1, :M], w_mx[:R, 1, M:].bitcast(U8), wd_bf[:])
         nc.sync.dma_start(out=w_mx[R : 2 * R], in_=w_mx[:R])
-        nc.sync.dma_start(out=xs_b[0][:], in_=xs_packed[:, 0:2, A:])
-        nc.sync.dma_start(out=x1_a[0][:], in_=x1_plain[:, 0::2, :A])
+        for a in range(2):
+            nc.sync.dma_start(out=x1_a[a][:], in_=x1_plain[:, a::2, :A])
 
-        for t in range(2):
-            interleave(nc.scalar.copy, xb_bf[t][:], x_raw[:, :, A + C * t : A + C * (t + 1)])
+        interleave(nc.scalar.copy, xb_bf[0][:], x_raw[:, :, A : A + C])
+        interleave(nc.scalar.copy, xb_bf[1][:, : C - X_VECTOR, :], x_raw[:, :, A + C : N - X_VECTOR])
         interleave(nc.vector.tensor_copy, xa_bf[:], x_raw[:, :, :A])
+        interleave(nc.vector.tensor_copy, xb_bf[1][:, C - X_VECTOR :, :], x_raw[:, :, N - X_VECTOR :])
 
         def quantize_and_copy(t):
             quantize(xb_mx[t][:, :C], xb_mx[t][:, C:].bitcast(U8), xb_bf[t][:])
@@ -160,15 +163,15 @@ def tile_rows_pl_mix_hyena_kernel(tc, x, w, dd, xs, x1, out_0, out_1, out_2):
                     wz_scales[rows, first_scale : first_scale + M // 4].bitcast(U8),
                     xb_copy[t][g][rows, :C], xb_copy[t][g][rows, C:].bitcast(U8), start, stop)
 
-        quantize_and_copy(0)
         quantize(xa_codes[:], xa_scales[:], xa_bf[:])
+        quantize_and_copy(0)
         for pair in (ORDER[:2], ORDER[2:]):
             for c in range(A // C):
                 for g in pair:
                     plain_pass(g, c)
         quantize_and_copy(1)
-        nc.sync.dma_start(out=x1_a[1][:], in_=x1_plain[:, 1::2, :A])
-        nc.sync.dma_start(out=xs_b[1][:], in_=xs_packed[:, 2:4, A:])
+        for h in range(2):
+            nc.sync.dma_start(out=xs_b[h][:], in_=xs_packed[:, 2 * h : 2 * h + 2, A:])
         for h in range(2):
             nc.sync.dma_start(out=x1_b[h][:], in_=x1_packed[:, 2 * h : 2 * h + 2, A:])
         nc.scalar.copy(
@@ -179,44 +182,73 @@ def tile_rows_pl_mix_hyena_kernel(tc, x, w, dd, xs, x1, out_0, out_1, out_2):
             out=wz_scales[:, 16:80].bitcast(U32).rearrange("p (u r i) -> p u r i", u=PACK, r=2),
             in_=w_mx[: 2 * R, 1, M:].bitcast(U32).rearrange("p (u i) -> p u i", u=PACK).unsqueeze(2).to_broadcast([2 * R, PACK, 2, 8]),
         )
-        binary(MULT, direct[:], xs_a[:], dd_all[:, :A].unsqueeze(1).to_broadcast([P, G, A]))
-        dd_b = dd_all[:, A:].unsqueeze(1).to_broadcast([P, 2, B])
-        nc.gpsimd.tensor_tensor(out=xs_a[:, 0:2, :], in0=xs_b[0][:], in1=dd_b, op=MULT)
-        direct_pair = (xs_a[:, 0:2, :], direct_b[:])
+        binary(MULT, direct[:, 0::2, :], xs_a[:, 0::2, :], dd_all[:, :A].unsqueeze(1).to_broadcast([P, 2, A]))
+        binary(MULT, direct[:, 1, :], xs_a[:, 1, :], dd_all[:, :A])
+        nc.gpsimd.tensor_tensor(out=xs_a[:, 0, :], in0=xs_a[:, G - 1, :], in1=dd_all[:, :A], op=MULT)
         for u in range(PACK):
             for t in range(2):
                 padded_pass(t, t, u, u % 2 == 0, False)
-        for h in range(2):
-            for step in range(1, G):
+        for step in range(1, G):
+            for h in range(2):
                 for e in range(2):
                     for t in range(2):
                         padded_pass(t, (t + step) % G, 2 * h + e, False, (step, e) == (G - 1, 1))
 
-        for g in ORDER:
-            binary(ADD, summed[:, g, :], z[g][:, :A], direct[:, g, :])
+        def add_plain(g):
+            binary(ADD, summed[:, g, :], z[g][:, :A], xs_a[:, 0, :] if g == G - 1 else direct[:, g, :])
+
+        for g in ORDER[:-1]:
+            add_plain(g)
         for g in ORDER:
             binary(MULT, y_a[:, g, :], summed[:, g, :], x1_a[g % 2][:, g // 2, :])
+            if g == ORDER[0]:
+                add_plain(ORDER[-1])
             nc.scalar.copy(out=y_bf[g][:], in_=y_a[:, g, :])
             nc.sync.dma_start(out=y_moved[R * g : R * (g + 1)], in_=y_bf[g][:])
         nc.sync.dma_start(out=y_plain[:, :, :A], in_=y_a[:])
-        interleave(nc.scalar.copy, y_words[0][:], y_moved[:])
+        interleave(nc.scalar.copy, y_words[0][:, : A - Y_VECTOR, :], y_moved[:, :, : A - Y_VECTOR])
 
-        binary(MULT, direct_b[:], xs_b[1][:], dd_b)
-        units = [(h, slice(2 * h, 2 * h + 2), t, slice(C * t, C * (t + 1))) for h in range(2) for t in range(2)]
-        for h, us, t, cols in units:
-            binary(ADD, summed_b[:, us, cols], z_b[h][t][:, : 2 * C].rearrange("p (e n) -> p e n", e=2), direct_pair[h][:, :, cols])
-        for h, us, t, cols in units:
-            engine = nc.gpsimd if (h, t) == (0, 0) else nc.vector
-            engine.tensor_tensor(out=y_b[:, us, cols], in0=summed_b[:, us, cols], in1=x1_b[h][:, :, cols], op=MULT)
+        def unit(h, t):
+            return slice(2 * h, 2 * h + 2), slice(C * t, C * (t + 1))
+
+        def factor(cols):
+            return dd_all[:, A:][:, cols].unsqueeze(1).to_broadcast([P, 2, cols.stop - cols.start])
+
+        def direct_of(h, t):
+            us, cols = unit(h, t)
+            return xs_b[0][:, :, cols] if (h, t) == (1, 1) else direct_b[:, us, cols]
+
+        def add_packed(h, t):
+            us, cols = unit(h, t)
+            binary(ADD, summed_b[:, us, cols], z_b[h][t][:, : 2 * C].rearrange("p (e n) -> p e n", e=2), direct_of(h, t))
+
+        def gate_packed(h, t):
+            us, cols = unit(h, t)
+            binary(MULT, y_b[:, us, cols], summed_b[:, us, cols], x1_b[h][:, :, cols])
             if t == 1:
                 nc.sync.dma_start(out=y_packed[:, us, A:], in_=y_b[:, us, :])
+
+        binary(MULT, direct_b[:, 0:2, :], xs_b[0][:], factor(slice(0, B)))
+        binary(MULT, direct_of(1, 0), xs_b[1][:, :, :C], factor(slice(0, C)))
+        nc.gpsimd.tensor_tensor(out=direct_of(1, 1), in0=xs_b[1][:, :, C:], in1=factor(slice(C, B)), op=MULT)
+        add_packed(0, 0)
+        add_packed(0, 1)
+        add_packed(1, 0)
+        gate_packed(0, 0)
+        add_packed(1, 1)
+        gate_packed(0, 1)
+        gate_packed(1, 0)
+        gate_packed(1, 1)
         for t in range(2):
             cols = slice(C * t, C * (t + 1))
             interleave(nc.vector.tensor_copy, y_words[1][:, cols, :], y_b[:, :, cols])
+        interleave(nc.vector.tensor_copy, y_words[0][:, A - Y_VECTOR :, :], y_moved[:, :, A - Y_VECTOR :])
+        for t in range(2):
+            cols = slice(C * t, C * (t + 1))
+            quantize(y_codes[1][:, cols], y_scales[:, A + C * t : A + C * (t + 1)], y_words[1][:, cols, :])
+        nc.sync.dma_start(out=words_out[:, A:], in_=y_codes[1][:])
         quantize(y_codes[0][:], y_scales[:, :A], y_words[0][:])
         nc.sync.dma_start(out=words_out[:, :A], in_=y_codes[0][:])
-        quantize(y_codes[1][:], y_scales[:, A:], y_words[1][:])
-        nc.sync.dma_start(out=words_out[:, A:], in_=y_codes[1][:])
         for q in range(G):
             queue = nc.scalar if q % 2 == 0 else nc.sync
             queue.dma_start(out=scales_out[4 * q : 4 * q + 4, :], in_=y_scales[R * q : R * q + 4, :].bitcast(I32))

@@ -75,10 +75,11 @@ def tile_rows_pl_mix_hyena_kernel(tc, x, w, dd, xs, x1, out_0, out_1, out_2):
             [xb_mx[t] if g == t else tile("xb_copy%d_%d" % (t, g), [2 * R, MX], I32) for g in range(G)] for t in range(2)
         ]
         xs_a = tile("xs_a", [P, G, A], F32)
-        x1_a = [tile("x1_a%d" % a, [P, 2, A], F32) for a in range(2)]
-        xs_b = [tile("xs_b%d" % h, [P, 2, B], F32) for h in range(2)]
+        x1_a = tile("x1_a", [P, G, A], F32)
+        xs_places = (slice(0, PACK - 1), slice(PACK - 1, PACK))
+        xs_b = [tile("xs_b%d" % i, [P, us.stop - us.start, B], F32) for i, us in enumerate(xs_places)]
         x1_b = [tile("x1_b%d" % h, [P, 2, B], F32) for h in range(2)]
-        direct = tile("direct", [P, G - 1, A], F32)
+        direct = tile("direct", [P, G, A], F32)
         summed = tile("summed", [P, G, A], F32)
         y_a = tile("y_a", [P, G, A], F32)
         y_bf = [tile("y_bf%d" % g, [P, A], BF16) for g in range(G)]
@@ -134,8 +135,7 @@ def tile_rows_pl_mix_hyena_kernel(tc, x, w, dd, xs, x1, out_0, out_1, out_2):
             queue.dma_start(out=w_mx[R * g : R * (g + 1), 0, :], in_=w_mx[:R, 0, :])
         quantize(w_mx[:R, 1, :M], w_mx[:R, 1, M:].bitcast(U8), wd_bf[:])
         nc.sync.dma_start(out=w_mx[R : 2 * R], in_=w_mx[:R])
-        for a in range(2):
-            nc.sync.dma_start(out=x1_a[a][:], in_=x1_plain[:, a::2, :A])
+        nc.sync.dma_start(out=x1_a[:], in_=x1_plain[:, :, :A])
 
         interleave(nc.scalar.copy, xb_bf[0][:], x_raw[:, :, A : A + C])
         interleave(nc.scalar.copy, xb_bf[1][:, : C - X_VECTOR, :], x_raw[:, :, A + C : N - X_VECTOR])
@@ -146,8 +146,7 @@ def tile_rows_pl_mix_hyena_kernel(tc, x, w, dd, xs, x1, out_0, out_1, out_2):
             quantize(xb_mx[t][:, :C], xb_mx[t][:, C:].bitcast(U8), xb_bf[t][:])
             for step in range(1, G):
                 g = (t + step) % G
-                queue = nc.gpsimd if (t, step) == (0, G - 1) else nc.sync
-                queue.dma_start(out=xb_copy[t][g][R * t : R * (t + 1)], in_=xb_mx[t][R * g : R * (g + 1)])
+                nc.sync.dma_start(out=xb_copy[t][g][R * t : R * (t + 1)], in_=xb_mx[t][R * g : R * (g + 1)])
 
         def plain_pass(g, c):
             rows = slice(R * g, R * (g + 1))
@@ -170,8 +169,8 @@ def tile_rows_pl_mix_hyena_kernel(tc, x, w, dd, xs, x1, out_0, out_1, out_2):
                 for g in pair:
                     plain_pass(g, c)
         quantize_and_copy(1)
-        for h in range(2):
-            nc.sync.dma_start(out=xs_b[h][:], in_=xs_packed[:, 2 * h : 2 * h + 2, A:])
+        for i, us in enumerate(xs_places):
+            nc.sync.dma_start(out=xs_b[i][:], in_=xs_packed[:, us, A:])
         for h in range(2):
             nc.sync.dma_start(out=x1_b[h][:], in_=x1_packed[:, 2 * h : 2 * h + 2, A:])
         nc.scalar.copy(
@@ -183,8 +182,7 @@ def tile_rows_pl_mix_hyena_kernel(tc, x, w, dd, xs, x1, out_0, out_1, out_2):
             in_=w_mx[: 2 * R, 1, M:].bitcast(U32).rearrange("p (u i) -> p u i", u=PACK).unsqueeze(2).to_broadcast([2 * R, PACK, 2, 8]),
         )
         binary(MULT, direct[:, 0::2, :], xs_a[:, 0::2, :], dd_all[:, :A].unsqueeze(1).to_broadcast([P, 2, A]))
-        binary(MULT, direct[:, 1, :], xs_a[:, 1, :], dd_all[:, :A])
-        nc.gpsimd.tensor_tensor(out=xs_a[:, 0, :], in0=xs_a[:, G - 1, :], in1=dd_all[:, :A], op=MULT)
+        binary(MULT, direct[:, 1::2, :], xs_a[:, 1::2, :], dd_all[:, :A].unsqueeze(1).to_broadcast([P, 2, A]))
         for u in range(PACK):
             for t in range(2):
                 padded_pass(t, t, u, u % 2 == 0, False)
@@ -195,12 +193,12 @@ def tile_rows_pl_mix_hyena_kernel(tc, x, w, dd, xs, x1, out_0, out_1, out_2):
                         padded_pass(t, (t + step) % G, 2 * h + e, False, (step, e) == (G - 1, 1))
 
         def add_plain(g):
-            binary(ADD, summed[:, g, :], z[g][:, :A], xs_a[:, 0, :] if g == G - 1 else direct[:, g, :])
+            binary(ADD, summed[:, g, :], z[g][:, :A], direct[:, g, :])
 
         for g in ORDER[:-1]:
             add_plain(g)
         for g in ORDER:
-            binary(MULT, y_a[:, g, :], summed[:, g, :], x1_a[g % 2][:, g // 2, :])
+            binary(MULT, y_a[:, g, :], summed[:, g, :], x1_a[:, g, :])
             if g == ORDER[0]:
                 add_plain(ORDER[-1])
             nc.scalar.copy(out=y_bf[g][:], in_=y_a[:, g, :])
@@ -211,16 +209,9 @@ def tile_rows_pl_mix_hyena_kernel(tc, x, w, dd, xs, x1, out_0, out_1, out_2):
         def unit(h, t):
             return slice(2 * h, 2 * h + 2), slice(C * t, C * (t + 1))
 
-        def factor(cols):
-            return dd_all[:, A:][:, cols].unsqueeze(1).to_broadcast([P, 2, cols.stop - cols.start])
-
-        def direct_of(h, t):
-            us, cols = unit(h, t)
-            return xs_b[0][:, :, cols] if (h, t) == (1, 1) else direct_b[:, us, cols]
-
         def add_packed(h, t):
             us, cols = unit(h, t)
-            binary(ADD, summed_b[:, us, cols], z_b[h][t][:, : 2 * C].rearrange("p (e n) -> p e n", e=2), direct_of(h, t))
+            binary(ADD, summed_b[:, us, cols], z_b[h][t][:, : 2 * C].rearrange("p (e n) -> p e n", e=2), direct_b[:, us, cols])
 
         def gate_packed(h, t):
             us, cols = unit(h, t)
@@ -228,9 +219,9 @@ def tile_rows_pl_mix_hyena_kernel(tc, x, w, dd, xs, x1, out_0, out_1, out_2):
             if t == 1:
                 nc.sync.dma_start(out=y_packed[:, us, A:], in_=y_b[:, us, :])
 
-        binary(MULT, direct_b[:, 0:2, :], xs_b[0][:], factor(slice(0, B)))
-        binary(MULT, direct_of(1, 0), xs_b[1][:, :, :C], factor(slice(0, C)))
-        nc.gpsimd.tensor_tensor(out=direct_of(1, 1), in0=xs_b[1][:, :, C:], in1=factor(slice(C, B)), op=MULT)
+        for i, us in enumerate(xs_places):
+            factor = dd_all[:, A:].unsqueeze(1).to_broadcast([P, us.stop - us.start, B])
+            binary(MULT, direct_b[:, us, :], xs_b[i][:], factor)
         add_packed(0, 0)
         add_packed(0, 1)
         add_packed(1, 0)

@@ -21,7 +21,6 @@ C = 128
 A = 2 * C
 B = N - A
 X_VECTOR = 64
-Y_VECTOR = 40
 MX = C + C // 4
 PAD = M - R
 ORDER = (0, 2, 1, 3)
@@ -76,13 +75,12 @@ def tile_rows_pl_mix_hyena_kernel(tc, x, w, dd, xs, x1, out_0, out_1, out_2):
         ]
         xs_a = tile("xs_a", [P, G, A], F32)
         x1_a = tile("x1_a", [P, G, A], F32)
-        xs_places = (slice(0, PACK - 1), slice(PACK - 1, PACK))
-        xs_b = [tile("xs_b%d" % i, [P, us.stop - us.start, B], F32) for i, us in enumerate(xs_places)]
-        x1_b = [tile("x1_b%d" % h, [P, 2, B], F32) for h in range(2)]
+        xs_b = tile("xs_b", [P, PACK, B], F32)
+        x1_b = tile("x1_b", [P, PACK, B], F32)
         direct = tile("direct", [P, G, A], F32)
         summed = tile("summed", [P, G, A], F32)
         y_a = tile("y_a", [P, G, A], F32)
-        y_bf = [tile("y_bf%d" % g, [P, A], BF16) for g in range(G)]
+        y_bf = tile("y_bf", [P, G, A], BF16)
         y_moved = tile("y_moved", [P, PACK, A], BF16)
         direct_b = tile("direct_b", [P, PACK, B], F32)
         summed_b = tile("summed_b", [P, PACK, B], F32)
@@ -91,7 +89,7 @@ def tile_rows_pl_mix_hyena_kernel(tc, x, w, dd, xs, x1, out_0, out_1, out_2):
         y_codes = [tile("y_codes%d" % h, [P, A], I32) for h in range(2)]
         y_scales = tile("y_scales", [P, N], U8)
         z = [ps.tile([P, N], F32, name="z%d" % g) for g in range(G)]
-        z_b = [[ps.tile([P, N], F32, name="z_b%d_%d" % (h, t)) for t in range(2)] for h in range(2)]
+        z_b = [ps.tile([P, N], F32, name="z_b%d" % t) for t in range(2)]
 
         def quantize(codes, scales, src):
             nc.vector.quantize_mx(out=codes.bitcast(FP8X4), scales=scales, in_=src.rearrange("p c j -> p (c j)"))
@@ -158,7 +156,7 @@ def tile_rows_pl_mix_hyena_kernel(tc, x, w, dd, xs, x1, out_0, out_1, out_2):
             rows = slice(R * t, R * (t + 1))
             first = PAD + M * u - R * g
             first_scale = 16 + 16 * u - 16 * (g // 2)
-            product(z_b[u // 2][t][:, C * (u % 2) : C * (u % 2 + 1)], wz_codes[rows, first : first + M],
+            product(z_b[t][:, C * u : C * (u + 1)], wz_codes[rows, first : first + M],
                     wz_scales[rows, first_scale : first_scale + M // 4].bitcast(U8),
                     xb_copy[t][g][rows, :C], xb_copy[t][g][rows, C:].bitcast(U8), start, stop)
 
@@ -169,10 +167,8 @@ def tile_rows_pl_mix_hyena_kernel(tc, x, w, dd, xs, x1, out_0, out_1, out_2):
                 for g in pair:
                     plain_pass(g, c)
         quantize_and_copy(1)
-        for i, us in enumerate(xs_places):
-            nc.sync.dma_start(out=xs_b[i][:], in_=xs_packed[:, us, A:])
-        for h in range(2):
-            nc.sync.dma_start(out=x1_b[h][:], in_=x1_packed[:, 2 * h : 2 * h + 2, A:])
+        nc.sync.dma_start(out=xs_b[:], in_=xs_packed[:, :, A:])
+        nc.sync.dma_start(out=x1_b[:], in_=x1_packed[:, :, A:])
         nc.scalar.copy(
             out=wz_codes[:, PAD:].bitcast(U32).rearrange("p (u m) -> p u m", u=PACK)[:, :, :R],
             in_=w_mx[: 2 * R, 1, :M].bitcast(U32).rearrange("p (u i) -> p u i", u=PACK),
@@ -185,61 +181,43 @@ def tile_rows_pl_mix_hyena_kernel(tc, x, w, dd, xs, x1, out_0, out_1, out_2):
         binary(MULT, direct[:, 1::2, :], xs_a[:, 1::2, :], dd_all[:, :A].unsqueeze(1).to_broadcast([P, 2, A]))
         for u in range(PACK):
             for t in range(2):
-                padded_pass(t, t, u, u % 2 == 0, False)
+                padded_pass(t, t, u, u == 0, False)
         for step in range(1, G):
-            for h in range(2):
-                for e in range(2):
-                    for t in range(2):
-                        padded_pass(t, (t + step) % G, 2 * h + e, False, (step, e) == (G - 1, 1))
+            for u in range(PACK):
+                for t in range(2):
+                    padded_pass(t, (t + step) % G, u, False, (step, u) == (G - 1, PACK - 1))
 
         def add_plain(g):
             binary(ADD, summed[:, g, :], z[g][:, :A], direct[:, g, :])
 
+        def gate_and_move(samples):
+            binary(MULT, y_a[:, samples, :], summed[:, samples, :], x1_a[:, samples, :])
+            for g in range(G)[samples]:
+                nc.scalar.copy(out=y_bf[:, g, :], in_=y_a[:, g, :])
+                nc.sync.dma_start(out=y_moved[R * g : R * (g + 1)], in_=y_bf[:, g, :])
+
         for g in ORDER[:-1]:
             add_plain(g)
-        for g in ORDER:
-            binary(MULT, y_a[:, g, :], summed[:, g, :], x1_a[:, g, :])
-            if g == ORDER[0]:
-                add_plain(ORDER[-1])
-            nc.scalar.copy(out=y_bf[g][:], in_=y_a[:, g, :])
-            nc.sync.dma_start(out=y_moved[R * g : R * (g + 1)], in_=y_bf[g][:])
+        gate_and_move(slice(0, G, 2))
+        add_plain(3)
+        for g in (1, 3):
+            gate_and_move(slice(g, g + 1))
         nc.sync.dma_start(out=y_plain[:, :, :A], in_=y_a[:])
-        interleave(nc.scalar.copy, y_words[0][:, : A - Y_VECTOR, :], y_moved[:, :, : A - Y_VECTOR])
+        interleave(nc.scalar.copy, y_words[0][:], y_moved[:])
 
-        def unit(h, t):
-            return slice(2 * h, 2 * h + 2), slice(C * t, C * (t + 1))
-
-        def add_packed(h, t):
-            us, cols = unit(h, t)
-            binary(ADD, summed_b[:, us, cols], z_b[h][t][:, : 2 * C].rearrange("p (e n) -> p e n", e=2), direct_b[:, us, cols])
-
-        def gate_packed(h, t):
-            us, cols = unit(h, t)
-            binary(MULT, y_b[:, us, cols], summed_b[:, us, cols], x1_b[h][:, :, cols])
-            if t == 1:
-                nc.sync.dma_start(out=y_packed[:, us, A:], in_=y_b[:, us, :])
-
-        for i, us in enumerate(xs_places):
-            factor = dd_all[:, A:].unsqueeze(1).to_broadcast([P, us.stop - us.start, B])
-            binary(MULT, direct_b[:, us, :], xs_b[i][:], factor)
-        add_packed(0, 0)
-        add_packed(0, 1)
-        add_packed(1, 0)
-        gate_packed(0, 0)
-        add_packed(1, 1)
-        gate_packed(0, 1)
-        gate_packed(1, 0)
-        gate_packed(1, 1)
-        for t in range(2):
-            cols = slice(C * t, C * (t + 1))
+        chunks = [slice(C * t, C * (t + 1)) for t in range(2)]
+        for cols in chunks:
+            binary(MULT, direct_b[:, :, cols], xs_b[:, :, cols], dd_all[:, A:][:, cols].unsqueeze(1).to_broadcast([P, PACK, C]))
+        for t, cols in enumerate(chunks):
+            binary(ADD, summed_b[:, :, cols], z_b[t][:].rearrange("p (u n) -> p u n", u=PACK), direct_b[:, :, cols])
+        for cols in chunks:
+            binary(MULT, y_b[:, :, cols], summed_b[:, :, cols], x1_b[:, :, cols])
+            nc.sync.dma_start(out=y_packed[:, :, A:][:, :, cols], in_=y_b[:, :, cols])
+        for cols in chunks:
             interleave(nc.vector.tensor_copy, y_words[1][:, cols, :], y_b[:, :, cols])
-        interleave(nc.vector.tensor_copy, y_words[0][:, A - Y_VECTOR :, :], y_moved[:, :, A - Y_VECTOR :])
-        for t in range(2):
-            cols = slice(C * t, C * (t + 1))
-            quantize(y_codes[1][:, cols], y_scales[:, A + C * t : A + C * (t + 1)], y_words[1][:, cols, :])
-        nc.sync.dma_start(out=words_out[:, A:], in_=y_codes[1][:])
-        quantize(y_codes[0][:], y_scales[:, :A], y_words[0][:])
-        nc.sync.dma_start(out=words_out[:, :A], in_=y_codes[0][:])
+        for h in range(2):
+            quantize(y_codes[h][:], y_scales[:, A * h : A * (h + 1)], y_words[h][:])
+            nc.sync.dma_start(out=words_out[:, A * h : A * (h + 1)], in_=y_codes[h][:])
         for q in range(G):
             queue = nc.scalar if q % 2 == 0 else nc.sync
             queue.dma_start(out=scales_out[4 * q : 4 * q + 4, :], in_=y_scales[R * q : R * q + 4, :].bitcast(I32))

@@ -21,6 +21,7 @@ C = 128
 A = 2 * C
 B = N - A
 X_VECTOR = 64
+Y_SCALAR = 64
 MX = C + C // 4
 PAD = M - R
 ORDER = (0, 2, 1, 3)
@@ -75,7 +76,8 @@ def tile_rows_pl_mix_hyena_kernel(tc, x, w, dd, xs, x1, out_0, out_1, out_2):
         ]
         xs_a = tile("xs_a", [P, G, A], F32)
         x1_a = tile("x1_a", [P, G, A], F32)
-        xs_b = tile("xs_b", [P, PACK, B], F32)
+        xs_places = (slice(0, PACK - 1), slice(PACK - 1, PACK))
+        xs_b = [tile("xs_b%d" % i, [P, us.stop - us.start, B], F32) for i, us in enumerate(xs_places)]
         x1_b = tile("x1_b", [P, PACK, B], F32)
         direct = tile("direct", [P, G, A], F32)
         summed = tile("summed", [P, G, A], F32)
@@ -89,7 +91,7 @@ def tile_rows_pl_mix_hyena_kernel(tc, x, w, dd, xs, x1, out_0, out_1, out_2):
         y_codes = [tile("y_codes%d" % h, [P, A], I32) for h in range(2)]
         y_scales = tile("y_scales", [P, N], U8)
         z = [ps.tile([P, N], F32, name="z%d" % g) for g in range(G)]
-        z_b = [ps.tile([P, N], F32, name="z_b%d" % t) for t in range(2)]
+        z_b = [[ps.tile([P, N], F32, name="z_b%d_%d" % (h, t)) for t in range(2)] for h in range(2)]
 
         def quantize(codes, scales, src):
             nc.vector.quantize_mx(out=codes.bitcast(FP8X4), scales=scales, in_=src.rearrange("p c j -> p (c j)"))
@@ -156,7 +158,7 @@ def tile_rows_pl_mix_hyena_kernel(tc, x, w, dd, xs, x1, out_0, out_1, out_2):
             rows = slice(R * t, R * (t + 1))
             first = PAD + M * u - R * g
             first_scale = 16 + 16 * u - 16 * (g // 2)
-            product(z_b[t][:, C * u : C * (u + 1)], wz_codes[rows, first : first + M],
+            product(z_b[u // 2][t][:, C * (u % 2) : C * (u % 2 + 1)], wz_codes[rows, first : first + M],
                     wz_scales[rows, first_scale : first_scale + M // 4].bitcast(U8),
                     xb_copy[t][g][rows, :C], xb_copy[t][g][rows, C:].bitcast(U8), start, stop)
 
@@ -167,7 +169,8 @@ def tile_rows_pl_mix_hyena_kernel(tc, x, w, dd, xs, x1, out_0, out_1, out_2):
                 for g in pair:
                     plain_pass(g, c)
         quantize_and_copy(1)
-        nc.sync.dma_start(out=xs_b[:], in_=xs_packed[:, :, A:])
+        for i, us in enumerate(xs_places):
+            nc.sync.dma_start(out=xs_b[i][:], in_=xs_packed[:, us, A:])
         nc.sync.dma_start(out=x1_b[:], in_=x1_packed[:, :, A:])
         nc.scalar.copy(
             out=wz_codes[:, PAD:].bitcast(U32).rearrange("p (u m) -> p u m", u=PACK)[:, :, :R],
@@ -181,11 +184,11 @@ def tile_rows_pl_mix_hyena_kernel(tc, x, w, dd, xs, x1, out_0, out_1, out_2):
         binary(MULT, direct[:, 1::2, :], xs_a[:, 1::2, :], dd_all[:, :A].unsqueeze(1).to_broadcast([P, 2, A]))
         for u in range(PACK):
             for t in range(2):
-                padded_pass(t, t, u, u == 0, False)
+                padded_pass(t, t, u, u % 2 == 0, False)
         for step in range(1, G):
             for u in range(PACK):
                 for t in range(2):
-                    padded_pass(t, (t + step) % G, u, False, (step, u) == (G - 1, PACK - 1))
+                    padded_pass(t, (t + step) % G, u, False, (step, u % 2) == (G - 1, 1))
 
         def add_plain(g):
             binary(ADD, summed[:, g, :], z[g][:, :A], direct[:, g, :])
@@ -206,15 +209,33 @@ def tile_rows_pl_mix_hyena_kernel(tc, x, w, dd, xs, x1, out_0, out_1, out_2):
         interleave(nc.scalar.copy, y_words[0][:], y_moved[:])
 
         chunks = [slice(C * t, C * (t + 1)) for t in range(2)]
+        pairs = [slice(2 * h, 2 * h + 2) for h in range(2)]
+
+        def add_packed(h, t):
+            bank = z_b[h][t][:, : 2 * C].rearrange("p (e n) -> p e n", e=2)
+            binary(ADD, summed_b[:, pairs[h], chunks[t]], bank, direct_b[:, pairs[h], chunks[t]])
+
+        def gate_packed(us, cols):
+            binary(MULT, y_b[:, us, cols], summed_b[:, us, cols], x1_b[:, us, cols])
+
+        for i, us in enumerate(xs_places):
+            factor = dd_all[:, A:].unsqueeze(1).to_broadcast([P, us.stop - us.start, B])
+            binary(MULT, direct_b[:, us, :], xs_b[i][:], factor)
+        add_packed(0, 0)
+        add_packed(0, 1)
+        add_packed(1, 0)
+        gate_packed(pairs[0], slice(0, B))
+        nc.sync.dma_start(out=y_packed[:, pairs[0], A:], in_=y_b[:, pairs[0], :])
+        add_packed(1, 1)
         for cols in chunks:
-            binary(MULT, direct_b[:, :, cols], xs_b[:, :, cols], dd_all[:, A:][:, cols].unsqueeze(1).to_broadcast([P, PACK, C]))
-        for t, cols in enumerate(chunks):
-            binary(ADD, summed_b[:, :, cols], z_b[t][:].rearrange("p (u n) -> p u n", u=PACK), direct_b[:, :, cols])
-        for cols in chunks:
-            binary(MULT, y_b[:, :, cols], summed_b[:, :, cols], x1_b[:, :, cols])
-            nc.sync.dma_start(out=y_packed[:, :, A:][:, :, cols], in_=y_b[:, :, cols])
-        for cols in chunks:
-            interleave(nc.vector.tensor_copy, y_words[1][:, cols, :], y_b[:, :, cols])
+            gate_packed(pairs[1], cols)
+        nc.sync.dma_start(out=y_packed[:, pairs[1], A:], in_=y_b[:, pairs[1], :])
+        for engine_copy, cols in (
+            (nc.vector.tensor_copy, slice(0, C)),
+            (nc.vector.tensor_copy, slice(C, B - Y_SCALAR)),
+            (nc.scalar.copy, slice(B - Y_SCALAR, B)),
+        ):
+            interleave(engine_copy, y_words[1][:, cols, :], y_b[:, :, cols])
         for h in range(2):
             quantize(y_codes[h][:], y_scales[:, A * h : A * (h + 1)], y_words[h][:])
             nc.sync.dma_start(out=words_out[:, A * h : A * (h + 1)], in_=y_codes[h][:])

from contextlib import ExitStack

import concourse.mybir as mybir

G, D, M, N = 4, 128, 128, 512
FLOPS = 2 * G * D * M * N

F32 = mybir.dt.float32
BF16 = mybir.dt.bfloat16
I32 = mybir.dt.int32
U32 = mybir.dt.uint32
U8 = mybir.dt.uint8
FP8X4 = mybir.dt.float8_e4m3fn_x4
ADD = mybir.AluOpType.add
MULT = mybir.AluOpType.mult

P = 128
R = 32
PACK = 4
C = 128
A = 2 * C
B = N - A
X_VECTOR = 64
Y_SCALAR = 64
MX = C + C // 4
PAD = M - R
ORDER = (0, 2, 1, 3)


def interleave(engine_copy, dst, src):
    engine_copy(
        out=dst.rearrange("p (c i) j -> p c j i", i=4),
        in_=src.rearrange("p j (c i) -> p c j i", i=4),
    )


def tile_rows_pl_mix_hyena_kernel(tc, x, w, dd, xs, x1, out_0, out_1, out_2):
    nc = tc.nc
    x_rows = x.rearrange("g (p j) n -> (g p) j n", j=PACK)
    w_rows = w.rearrange("(p j) m -> p j m", j=PACK)
    xs_plain = xs.rearrange("g m n -> m g n")
    x1_plain = x1.rearrange("g m n -> m g n")
    y_plain = out_0.rearrange("(g m) n -> m g n", g=G)
    xs_packed = xs.rearrange("g (p u) n -> (g p) u n", u=PACK)
    x1_packed = x1.rearrange("g (p u) n -> (g p) u n", u=PACK)
    y_packed = out_0.rearrange("(p u) n -> p u n", u=PACK)
    words_out = out_1.rearrange("v p n u -> (v p) (n u)").bitcast(I32)
    scales_out = out_2.rearrange("v f n -> (v f) n").bitcast(I32)

    with ExitStack() as ctx:
        sb = ctx.enter_context(tc.tile_pool(name="sb", bufs=1))
        ps = ctx.enter_context(tc.psum_pool(name="ps", bufs=1))
        ctx.enter_context(tc.manual_schedule())

        def tile(name, shape, dtype):
            return sb.tile(shape, dtype, name=name, align_bytes=256)

        w_raw = tile("w_raw", [R, PACK, M], F32)
        w_bf = tile("w_bf", [R, M, PACK], BF16)
        wd_bf = tile("wd_bf", [R, M, PACK], BF16)
        w_mx = tile("w_mx", [P, 2, MX], I32)
        wz_codes = tile("wz_codes", [2 * R, PAD + PACK * M], I32)
        wz_scales = tile("wz_scales", [2 * R, 96], I32)
        dd_rows = tile("dd_rows", [P, R], F32)
        dd_cols = tile("dd_cols", [P, R], F32)
        dd_wide = tile("dd_wide", [P, N], F32)
        dd_all = tile("dd_all", [P, N], F32)
        x_raw = tile("x_raw", [P, PACK, N], F32)
        xa_bf = tile("xa_bf", [P, A, PACK], BF16)
        xb_bf = [tile("xb_bf%d" % t, [P, C, PACK], BF16) for t in range(2)]
        xa_codes = tile("xa_codes", [P, A], I32)
        xa_scales = tile("xa_scales", [P, A], U8)
        xb_mx = [tile("xb_mx%d" % t, [P, MX], I32) for t in range(2)]
        xb_copy = [
            [xb_mx[t] if g == t else tile("xb_copy%d_%d" % (t, g), [2 * R, MX], I32) for g in range(G)] for t in range(2)
        ]
        xs_a = tile("xs_a", [P, G, A], F32)
        x1_a = tile("x1_a", [P, G, A], F32)
        xs_places = (slice(0, PACK - 1), slice(PACK - 1, PACK))
        xs_b = [tile("xs_b%d" % i, [P, us.stop - us.start, B], F32) for i, us in enumerate(xs_places)]
        x1_b = tile("x1_b", [P, PACK, B], F32)
        direct = tile("direct", [P, G, A], F32)
        summed = tile("summed", [P, G, A], F32)
        y_a = tile("y_a", [P, G, A], F32)
        y_bf = tile("y_bf", [P, G, A], BF16)
        y_moved = tile("y_moved", [P, PACK, A], BF16)
        direct_b = tile("direct_b", [P, PACK, B], F32)
        summed_b = tile("summed_b", [P, PACK, B], F32)
        y_b = tile("y_b", [P, PACK, B], F32)
        y_words = [tile("y_words%d" % h, [P, A, PACK], BF16) for h in range(2)]
        y_codes = [tile("y_codes%d" % h, [P, A], I32) for h in range(2)]
        y_scales = tile("y_scales", [P, N], U8)
        z = [ps.tile([P, N], F32, name="z%d" % g) for g in range(G)]
        z_b = [[ps.tile([P, N], F32, name="z_b%d_%d" % (h, t)) for t in range(2)] for h in range(2)]

        def quantize(codes, scales, src):
            nc.vector.quantize_mx(out=codes.bitcast(FP8X4), scales=scales, in_=src.rearrange("p c j -> p (c j)"))

        def product(out, w_c, w_s, x_c, x_s, start, stop):
            nc.tensor.matmul_mx(
                out=out, lhsT=w_c.bitcast(FP8X4), lhsT_scale=w_s, rhs=x_c.bitcast(FP8X4), rhs_scale=x_s,
                start=start, stop=stop,
            )

        def binary(op, out, in0, in1):
            nc.vector.tensor_tensor(out=out, in0=in0, in1=in1, op=op)

        nc.sync.dma_start(out=w_raw[:], in_=w_rows)
        nc.scalar.dma_start(
            out=dd_rows[:],
            in_=dd.rearrange("o (b i) -> o b i", i=R).broadcast_to([P // 16, 16, R]),
        )
        nc.sync.dma_start(out=x_raw[:], in_=x_rows)
        nc.sync.dma_start(out=xs_a[:], in_=xs_plain[:, :, :A])

        nc.vector.memset(w_mx[:R, :, M:], 0)
        for t in range(2):
            nc.vector.memset(xb_mx[t][:, C:], 0)
        nc.vector.memset(wz_codes[:], 0)
        nc.vector.memset(wz_scales[:], 0)
        nc.vector.transpose(out=dd_cols[:], in_=dd_rows[:])
        interleave(nc.scalar.copy, w_bf[:], w_raw[:])
        nc.vector.tensor_copy(
            out=dd_wide[:].rearrange("p (b i) -> p b i", i=R),
            in_=dd_cols[:, 0:16].unsqueeze(2).to_broadcast([P, 16, R]),
        )
        nc.scalar.copy(
            out=wd_bf[:].rearrange("p (u i) j -> p u i j", u=PACK),
            in_=w_raw[:].rearrange("p j (i u) -> p u i j", u=PACK),
        )
        nc.vector.transpose(out=dd_all[:], in_=dd_wide[:])
        quantize(w_mx[:R, 0, :M], w_mx[:R, 0, M:].bitcast(U8), w_bf[:])
        for g in (2, 3):
            queue = nc.scalar if g == 2 else nc.sync
            queue.dma_start(out=w_mx[R * g : R * (g + 1), 0, :], in_=w_mx[:R, 0, :])
        quantize(w_mx[:R, 1, :M], w_mx[:R, 1, M:].bitcast(U8), wd_bf[:])
        nc.sync.dma_start(out=w_mx[R : 2 * R], in_=w_mx[:R])
        nc.sync.dma_start(out=x1_a[:], in_=x1_plain[:, :, :A])

        interleave(nc.scalar.copy, xb_bf[0][:], x_raw[:, :, A : A + C])
        interleave(nc.scalar.copy, xb_bf[1][:, : C - X_VECTOR, :], x_raw[:, :, A + C : N - X_VECTOR])
        interleave(nc.vector.tensor_copy, xa_bf[:], x_raw[:, :, :A])
        interleave(nc.vector.tensor_copy, xb_bf[1][:, C - X_VECTOR :, :], x_raw[:, :, N - X_VECTOR :])

        def quantize_and_copy(t):
            quantize(xb_mx[t][:, :C], xb_mx[t][:, C:].bitcast(U8), xb_bf[t][:])
            for step in range(1, G):
                g = (t + step) % G
                nc.sync.dma_start(out=xb_copy[t][g][R * t : R * (t + 1)], in_=xb_mx[t][R * g : R * (g + 1)])

        def plain_pass(g, c):
            rows = slice(R * g, R * (g + 1))
            cols = slice(C * c, C * (c + 1))
            product(z[g][:, cols], w_mx[rows, 0, :M], w_mx[rows, 0, M:].bitcast(U8),
                    xa_codes[rows, cols], xa_scales[rows, cols], True, True)

        def padded_pass(t, g, u, start, stop):
            rows = slice(R * t, R * (t + 1))
            first = PAD + M * u - R * g
            first_scale = 16 + 16 * u - 16 * (g // 2)
            product(z_b[u // 2][t][:, C * (u % 2) : C * (u % 2 + 1)], wz_codes[rows, first : first + M],
                    wz_scales[rows, first_scale : first_scale + M // 4].bitcast(U8),
                    xb_copy[t][g][rows, :C], xb_copy[t][g][rows, C:].bitcast(U8), start, stop)

        quantize(xa_codes[:], xa_scales[:], xa_bf[:])
        quantize_and_copy(0)
        for pair in (ORDER[:2], ORDER[2:]):
            for c in range(A // C):
                for g in pair:
                    plain_pass(g, c)
        quantize_and_copy(1)
        for i, us in enumerate(xs_places):
            nc.sync.dma_start(out=xs_b[i][:], in_=xs_packed[:, us, A:])
        nc.sync.dma_start(out=x1_b[:], in_=x1_packed[:, :, A:])
        nc.scalar.copy(
            out=wz_codes[:, PAD:].bitcast(U32).rearrange("p (u m) -> p u m", u=PACK)[:, :, :R],
            in_=w_mx[: 2 * R, 1, :M].bitcast(U32).rearrange("p (u i) -> p u i", u=PACK),
        )
        nc.scalar.copy(
            out=wz_scales[:, 16:80].bitcast(U32).rearrange("p (u r i) -> p u r i", u=PACK, r=2),
            in_=w_mx[: 2 * R, 1, M:].bitcast(U32).rearrange("p (u i) -> p u i", u=PACK).unsqueeze(2).to_broadcast([2 * R, PACK, 2, 8]),
        )
        binary(MULT, direct[:, 0::2, :], xs_a[:, 0::2, :], dd_all[:, :A].unsqueeze(1).to_broadcast([P, 2, A]))
        binary(MULT, direct[:, 1::2, :], xs_a[:, 1::2, :], dd_all[:, :A].unsqueeze(1).to_broadcast([P, 2, A]))
        for u in range(PACK):
            for t in range(2):
                padded_pass(t, t, u, u % 2 == 0, False)
        for step in range(1, G):
            for u in range(PACK):
                for t in range(2):
                    padded_pass(t, (t + step) % G, u, False, (step, u % 2) == (G - 1, 1))

        def add_plain(g):
            binary(ADD, summed[:, g, :], z[g][:, :A], direct[:, g, :])

        def gate_and_move(samples):
            binary(MULT, y_a[:, samples, :], summed[:, samples, :], x1_a[:, samples, :])
            for g in range(G)[samples]:
                nc.scalar.copy(out=y_bf[:, g, :], in_=y_a[:, g, :])
                nc.sync.dma_start(out=y_moved[R * g : R * (g + 1)], in_=y_bf[:, g, :])

        for g in ORDER[:-1]:
            add_plain(g)
        gate_and_move(slice(0, G, 2))
        add_plain(3)
        for g in (1, 3):
            gate_and_move(slice(g, g + 1))
        nc.sync.dma_start(out=y_plain[:, :, :A], in_=y_a[:])
        interleave(nc.scalar.copy, y_words[0][:], y_moved[:])

        chunks = [slice(C * t, C * (t + 1)) for t in range(2)]
        pairs = [slice(2 * h, 2 * h + 2) for h in range(2)]

        def add_packed(h, t):
            bank = z_b[h][t][:, : 2 * C].rearrange("p (e n) -> p e n", e=2)
            binary(ADD, summed_b[:, pairs[h], chunks[t]], bank, direct_b[:, pairs[h], chunks[t]])

        def gate_packed(us, cols):
            binary(MULT, y_b[:, us, cols], summed_b[:, us, cols], x1_b[:, us, cols])

        for i, us in enumerate(xs_places):
            factor = dd_all[:, A:].unsqueeze(1).to_broadcast([P, us.stop - us.start, B])
            binary(MULT, direct_b[:, us, :], xs_b[i][:], factor)
        add_packed(0, 0)
        add_packed(0, 1)
        add_packed(1, 0)
        gate_packed(pairs[0], slice(0, B))
        nc.sync.dma_start(out=y_packed[:, pairs[0], A:], in_=y_b[:, pairs[0], :])
        add_packed(1, 1)
        for cols in chunks:
            gate_packed(pairs[1], cols)
        nc.sync.dma_start(out=y_packed[:, pairs[1], A:], in_=y_b[:, pairs[1], :])
        for engine_copy, cols in (
            (nc.vector.tensor_copy, slice(0, C)),
            (nc.vector.tensor_copy, slice(C, B - Y_SCALAR)),
            (nc.scalar.copy, slice(B - Y_SCALAR, B)),
        ):
            interleave(engine_copy, y_words[1][:, cols, :], y_b[:, :, cols])
        for h in range(2):
            quantize(y_codes[h][:], y_scales[:, A * h : A * (h + 1)], y_words[h][:])
            nc.sync.dma_start(out=words_out[:, A * h : A * (h + 1)], in_=y_codes[h][:])
        for q in range(G):
            queue = nc.scalar if q % 2 == 0 else nc.sync
            queue.dma_start(out=scales_out[4 * q : 4 * q + 4, :], in_=y_scales[R * q : R * q + 4, :].bitcast(I32))
